import numpy as np, ml_dtypes
CORES = [3,7,11,15,131,135,139,143]
N = 8
BF = ml_dtypes.bfloat16
def gentries(a):
    return np.ascontiguousarray(a.reshape(8, 16, -1).transpose(0, 2, 1)).reshape(8, -1)
def gtable(e):
    e = np.asarray(e); return np.ascontiguousarray(e.reshape(8, -1, 16).transpose(0, 2, 1)).reshape(128, -1).astype(np.int32)
V, K, RO, TH, NR, A = 1792, 256, 3, 12, 10, 1
EPS = 0.5
P = V // 16
def kinds(rng):
    i = np.arange(V); cut = rng.random(V) < 0.04; cut[0] = True
    last = np.maximum.accumulate(np.where(cut, i, 0)); v = rng.integers(0, P, V)
    return (v[last] + i - last) % P
def names(rng, kd):
    o = np.argsort(kd, kind="stable"); n = np.bincount(kd, minlength=P); s = np.add.accumulate(n) - n
    b = np.zeros((N, 8, 16, P), np.int64)
    for k in range(P):
        new = o[np.minimum(s[k] + (rng.random((N, 8, 16)) * n[k]).astype(np.int64), V - 1)]
        nxt = (b[..., k - 1] + 1) % V
        b[..., k] = np.where((kd[nxt] == k) & (rng.random((N, 8, 16)) < 0.85), nxt, new) if k else new
    return b
def blur(rng, r, lev):
    u = rng.random(r.shape, dtype=np.float32)
    r = np.where(u < lev, r + rng.integers(-3, 4, r.shape), r)
    return np.where(u < 0.3 * lev, rng.integers(0, V, r.shape), r) % V
def parts(rng, lev=(0.0, 0.15, 0.35, 0.8), dev=(0.1, 0.3, 0.6, 1.0)):
    kd = kinds(rng); b = names(rng, kd)
    r = blur(rng, b[..., kd], rng.choice(np.array(lev), (N, 8, 1, V)))
    x = rng.standard_normal((N, 8, 16, P), dtype=np.float32)[..., kd]
    x = x + rng.choice(np.array(dev), (N, 8, 1, V)).astype(np.float32) * rng.standard_normal((N, 8, 16, V), dtype=np.float32)
    return kd, b, x, r, rng.integers(0, V, (N, 8, K))
def pack(x, r, w):
    x = np.clip(x, -4.0, 4.0); x = np.where(np.abs(x) < 2.0 ** -19, 0.0, x)
    return {"x": np.ascontiguousarray(x.reshape(N, 128, V)).astype(np.float32).astype(BF), "rec": np.ascontiguousarray(r.reshape(N, 128, V)).astype(np.int32), "w0": np.stack([gtable(a) for a in w])}
def setup_inputs(rng):
    kd, b, x, r, w = parts(rng)
    return pack(x, r, w)
def setup_inputs_spread(rng):
    kd, b, x, r, w = parts(rng, (0.0, 0.05, 0.4, 1.0), (0.02, 0.1, 0.5, 1.2))
    x = x * np.exp2(rng.integers(-1, 2, (N, 8, 1, V))).astype(np.float32)
    far = (rng.random((N, 8, 1, V)) < 0.7) & (np.arange(N) % 2 == 1)[:, None, None, None]
    x = x + np.where(far, 2.5, 0.0).astype(np.float32) * rng.standard_normal((N, 8, 16, V), dtype=np.float32)
    w = np.minimum((V * rng.random((N, 8, K)) ** 2).astype(np.int64), V - 1)
    return pack(x, r, w)
def setup_inputs_ends(rng):
    kd, b, x, r, w = parts(rng)
    pat = rng.choice(np.array([0, V - 1]), (N, 8, 16, 1)); pat[:, :, 0] = 0; pat[:, :, 15] = V - 1
    val = np.where(rng.random(r.shape, dtype=np.float32) < 0.2, V - 1 - pat, pat); kind = rng.integers(0, 4, (N, 8, 1, V))
    val = np.where(kind == 0, 0, np.where(kind == 1, V - 1, val))
    r = np.where(rng.random((N, 8, 1, V)) < 0.78, val, r)
    x = np.where(rng.random((N, 8, 1, V)) < 0.78, np.where(x < 0, -4.0, 4.0), x)
    xp = rng.choice(np.array([-4.0, 4.0]), (N, 8, 16)); pl = pat[..., 0]
    o1 = np.argsort(rng.random((N, 8, 16)), axis=2); o2 = np.argsort(rng.random((N, 8, 16)), axis=2)
    for v in [V - 1] + list(range(RO + 2)):
        n1 = rng.choice(np.array([0, 0, 16 - TH, 16 - TH, 17 - TH, 16]), (N, 8, 1)); n2 = rng.choice(np.array([0, 16 - NR, 16 - NR, 17 - NR]), (N, 8, 1))
        if v == V - 1: n1 = n1 * 0; n2 = n2 * 0
        r[..., v] = np.where(o1 < n1, V - 1 - pl, pl); x[..., v] = np.where(o2 < n2, -xp, xp)
    w = np.where(rng.random((N, 8, K)) < 0.75, rng.choice(np.array([0, V - 1]), (N, 8, K)), w)
    w[..., 0] = V - 1; w[..., 1] = 0; w[..., K - 1] = V - 1
    return pack(x, r, w)
def setup_inputs_corners(rng):
    kd, b, x, r, w = parts(rng); i = np.arange(V)
    for q in range(N):
        o = rng.permutation(8)
        for g in range(8):
            if o[g] == 0: r[q, g] = i
            if o[g] == 1: r[q, g] = 0
            if o[g] == 2: r[q, g] = V - 1
            if 3 <= o[g] <= 5: r[q, g] = (i + (int(o[g]) - 2)) % V
    w = np.where(rng.random((N, 8, K)) < 0.5, rng.choice(np.array([0, 1, 2, V - 3, V - 2, V - 1]), (N, 8, K)), w)
    w[..., 0] = V - 1; w[..., K - 1] = V - 1
    return pack(x, r, w)
def setup_inputs_ties(rng):
    kd = kinds(rng); b = names(rng, kd); c = b[..., kd]
    o = np.argsort(rng.random(c.shape, dtype=np.float32), axis=2); kind = rng.choice(np.array([0, 1, 2]), (N, 8, 1, V), p=[0.5, 0.3, 0.2])
    far = np.where(kind == 0, 0, np.where(kind == 1, 16 - TH, 17 - TH)); sg = rng.choice(np.array([-1, 1]), (N, 8, 1, V))
    s = np.where(o < far, 3 * sg, np.where((kind > 0) & (o % 2 == 1), 2 * sg, 0))
    r = c + s; r = np.where((r < 0) | (r >= V), c - s, r)
    x = 0.25 * rng.integers(-8, 9, (N, 8, 16, P))[..., kd]
    o = np.argsort(rng.random(c.shape, dtype=np.float32), axis=2); kind = rng.choice(np.array([0, 1, 2]), (N, 8, 1, V), p=[0.4, 0.3, 0.3])
    far = np.where(kind == 1, 16 - NR, 17 - NR); sg = rng.choice(np.array([-1.0, 1.0]), c.shape)
    x = x + np.where(kind > 0, np.where(o < far, 0.515625, 0.5) * sg, 0.0)
    return pack(x, r, rng.integers(0, V, (N, 8, K)))
def setup_inputs_crowd(rng):
    kd, b, x, r, w = parts(rng, (0.0, 0.1, 0.2, 0.3)); r[:, :, 1] = b[:, :, 1][..., kd]
    for q in range(N):
        for g in range(8):
            k = (g + q) % 8; v = int(rng.integers(0, V)); mem = np.flatnonzero(kd == kd[v])
            if k < 4: w[q, g] = v
            if k == 2: w[q, g, K - 1] = mem[int(rng.integers(0, len(mem)))]
            if k == 3: w[q, g, 0] = mem[int(rng.integers(0, len(mem)))]
            if k == 4 or k == 5: w[q, g] = mem[rng.integers(0, len(mem), K)]
            if k == 6: w[q, g] = rng.choice(np.array([v, (v + 1) % V, V - 1]), K)
    return pack(x, r, w)
def check_ranges(d):
    bad = []
    for k in ("rec", "w0"):
        if np.min(d[k]) < 0 or np.max(d[k]) > V - 1: bad.append("range of " + k)
    a = np.abs(np.asarray(d["x"]).astype(np.float32))
    if not np.all((a == 0) | ((a >= 2.0 ** -19) & (a <= 4.0))): bad.append("range of x")
    return bad
def likeness(R, c, w):
    rc = np.take_along_axis(R, c.reshape(8, 1, 16 * K), 2).reshape(8, 16, 16, K)
    rw = np.take_along_axis(R, w[:, None, :], 2)[:, :, None, :]
    return np.add.reduce(np.abs(rc - rw) <= 2, axis=1, dtype=np.int32)
def reference(x, rec, w0):
    X = np.asarray(x).astype(np.float32).reshape(N, 8, 16, V); R = rec.astype(np.int32).reshape(N, 8, 16, V)
    w = np.stack([gentries(a) for a in w0]).astype(np.int32); ys = []
    for t in range(1, RO + 1):
        new = R.copy(); S = []; nxt = []
        for a in range(N):
            c = np.take_along_axis(R[a], w[a][:, None, :], 2)
            ok = likeness(R[a], c, w[a]) >= TH
            for b in range(A):
                q = (a + 1 + ((t - 1) * A + b) % (N - 1)) % N
                ok = ok & (likeness(R[q][(np.arange(8) + t + b) % 8], c, w[a]) >= TH)
            o = ok[:, (t + np.arange(16)) % 16]; has = np.any(o, axis=1); k = (t + np.argmax(o, axis=1)) % 16
            j = np.where(has, np.take_along_axis(c, k[:, None, :], 1)[:, 0], w[a])
            z = ((j + 1) % V).astype(np.int32); n = (c + 1) % V
            xn = np.take_along_axis(X[a], n.reshape(8, 1, 16 * K), 2).reshape(8, 16, 16, K)
            xz = np.take_along_axis(X[a], z[:, None, :], 2)[:, :, None, :]
            S.append(np.add.reduce(np.exp(-np.abs(xn.astype(np.float64) - xz.astype(np.float64))), axis=2))
            if t < RO:
                put = np.add.reduce(np.abs(xn - xz) <= np.float32(EPS), axis=1, dtype=np.int32) >= NR
                for g in range(8):
                    at = np.flatnonzero(has[g])
                    u, first = np.unique(z[g, at], return_index=True); lw = at[first]
                    new[a, g][:, u] = np.where(put[g][:, lw], n[g][:, lw], R[a, g][:, u])
            nxt.append(z)
        R = new; w = np.stack(nxt); ys.append(np.stack(S))
    return {"y": np.concatenate(ys, axis=3).reshape(N, 128, RO * K).astype(np.float32)}

def check_inputs(d):
    bad = list(check_ranges(d))
    if not bad:
        for name, y in reference(**d).items():
            for q in range(N):
                v = np.abs(np.asarray(y[q], np.float64)); s = np.sqrt(np.mean(v * v))
                if v.max() > 4 * s or s < 2.0 ** 1: bad.append('%s of rank %d is uneven or too small' % (name, q))
    return bad

@@ -1,0 +1,648 @@
+import math
+from concourse.bass import DstId, RemoteDMATransfer
+from concourse.mybir import AluOpType as Op, ActivationFunctionType as Fn
+
+V, K, RO, H = 1792, 256, 3, 128
+BIG = 4096.0
+C4 = 1.5 * 2.0 ** 25
+C1 = 1.5 * 2.0 ** 23
+LNB = 0.5 * math.log(3.0)
+NS_OWN = ((2, 1), (2, 1), (2, 1))
+EARLY = 1
+NS_NEAR = 3
+
+SCRATCH = {
+    "R": ("sbuf", [128, 2048], "int32"), "Rg": ("sbuf", [128, V], "int32"), "Xs": ("sbuf", [128, 2048], "bfloat16"),
+    "w0i": ("sbuf", [128, 16], "int32"),
+    "q0": ("sbuf", [128, 288], "uint16"), "q1": ("sbuf", [128, 288], "uint16"), "q2": ("sbuf", [128, 288], "uint16"),
+    "lq": ("sbuf", [128, 3 * 272], "uint16"), "an": ("sbuf", [128, 768], "bfloat16"), "la": ("sbuf", [128, 768], "bfloat16"),
+    "Rw": ("sbuf", [128, 272], "float32"), "R4": ("sbuf", [128, 1024], "float32"), "G4": ("sbuf", [128, 1024], "float32"),
+    "Tr": ("sbuf", [128, 512], "float32"),
+    "dO": ("sbuf", [128, 4096], "bfloat16"), "dG": ("sbuf", [128, 4096], "bfloat16"), "XC": ("sbuf", [128, 4096], "bfloat16"),
+    "A0": ("sbuf", [128, 4096], "float32"), "A1": ("sbuf", [128, 4096], "float32"),
+    "twin": ("sbuf", [128, K], "bfloat16"), "sel": ("sbuf", [128, K], "float16"), "key": ("sbuf", [128, K], "float16"),
+    "xz": ("sbuf", [128, K], "bfloat16"), "rr": ("sbuf", [128, K], "bfloat16"), "nn": ("sbuf", [128, K], "float32"),
+    "dl": ("sbuf", [128, K], "float32"), "nw": ("sbuf", [128, K], "float32"),
+    "win": ("sbuf", [128, K], "bfloat16"), "thr": ("sbuf", [128, K], "float32"),
+    "L": ("sbuf", [128, 256], "float32"), "Li": ("sbuf", [128, 32], "int32"), "Lu": ("sbuf", [128, 64], "uint16"),
+    "ss": ("sbuf", [128, 512], "float32"), "acc": ("sbuf", [128, 1024], "float32"), "yo": ("sbuf", [128, K], "float32"),
+    "J": ("sbuf", [128, 256], "float32"), "Km": ("sbuf", [128, 144], "float32"), "Gm": ("sbuf", [128, 128], "float32"),
+    "Wb": ("sbuf", [128, 256], "bfloat16"), "Wh": ("sbuf", [128, 256], "float16"), "Wl": ("sbuf", [128, 256], "bfloat16"),
+    "BDb": ("sbuf", [128, 128], "bfloat16"), "BDh": ("sbuf", [128, 128], "float16"),
+    "Ib": ("sbuf", [128, 128], "bfloat16"), "nIb": ("sbuf", [128, 128], "bfloat16"), "bIb": ("sbuf", [128, 128], "bfloat16"),
+    "If": ("sbuf", [128, 128], "float32"), "Tri": ("sbuf", [128, 384], "bfloat16"), "Tq": ("sbuf", [128, 128], "bfloat16"),
+    "P": ("psum", [128, 4096], "float32"),
+}
+NDMA = 16
+SEMAPHORES = (["sv", "sa", "st", "sg", "sent", "fold0", "fold1", "hin0", "hin1", "back0", "back1"]
+              + ["qa%d" % i for i in range(RO)] + ["aa%d" % i for i in range(2 * RO)] + ["d%d" % i for i in range(NDMA)])
+
+
+def helper_of(core, T, topo):
+    for c in topo.cores_of(core):
+        if c != core and T.rank_of(c) is None and topo.die(c) == topo.die(core):
+            return c
+    return None
+
+
+def bits(engines):
+    m = 0
+    for e in engines:
+        m |= 1 << e
+    return m
+
+
+def rank_program(g, core, T, topo):
+    rank = T.rank_of(core)
+    if rank is None:
+        for c in T.cores:
+            if helper_of(c, T, topo) == core:
+                hand_back(g, core, c, T, topo)
+        return
+    walk(g, core, rank, T, topo)
+
+
+def fold_engines(core, T, topo):
+    far = [c for c in T.cores if c not in topo.cores_of(core)][0]
+    return [e for e in topo.engines(core, helper_of(core, T, topo)) if e not in topo.engines(core, far)]
+
+
+def hand_back(g, core, owner, T, topo):
+    rid, pid = topo.addr(owner, core)
+    n = len(fold_engines(owner, T, topo))
+    m = topo.mask(core, owner)
+    for s in range(RO - 1):
+        g.wait_ge(T.sem["hin%d" % s], n)
+        g.remote_dma(T.ss[:, s * K:(s + 1) * K], T.ss[:, s * K:(s + 1) * K], T.sem["back%d" % s], T.sem.sent, pid, rid, m)
+    g.wait_ge(T.sem.sent, (RO - 1) * len(topo.engines(core, owner)))
+
+
+def walk(g, core, rank, T, topo):
+    N = len(T.cores)
+    eng = {"v": g.vector, "a": g.scalar, "t": g.tensor, "g": g, "s": g.sync}
+    own = {"v": "sv", "a": "sa", "t": "st", "g": "sg"}
+    count = {}
+    known = {q: {} for q in eng}
+    hist = {}
+    ndma = [0]
+
+    def need(q, sem, val, kn):
+        if known[q].get(sem, 0) >= val:
+            return
+        eng[q].wait_ge(T.sem[sem], val)
+        known[q][sem] = val
+        for s, n in kn.items():
+            if known[q].get(s, 0) < n:
+                known[q][s] = n
+
+    def order(q, reads, writes):
+        deps = []
+        for rs, w in ((reads, False), (writes, True)):
+            for name, lo, hi in rs:
+                for lo2, hi2, w2, q2, sem, val, kn in hist.get(name, []):
+                    if name == "P":
+                        if q2 != q:
+                            hit = lo // 512 <= (hi2 - 1) // 512 and lo2 // 512 <= (hi - 1) // 512
+                        else:
+                            hit = q != "t" and lo < hi2 and lo2 < hi and (w or w2)
+                    else:
+                        hit = lo < hi2 and lo2 < hi and (w or w2)
+                    if hit:
+                        deps.append((val, sem, kn))
+        deps.sort(key=lambda d: -d[0])
+        for val, sem, kn in deps:
+            need(q, sem, val, kn)
+
+    def note(q, sem, val, reads, writes):
+        kn = dict(known[q]) if q in known else {}
+        for rs, w in ((reads, False), (writes, True)):
+            for name, lo, hi in rs:
+                h = hist.setdefault(name, [])
+                if w:
+                    h[:] = [e for e in h if not (lo <= e[0] and e[1] <= hi and (name != "P" or e[3] == q))]
+                h.append((lo, hi, w, q, sem, val, kn))
+
+    def op(q, reads, writes, call):
+        order(q, reads, writes)
+        sem = own[q]
+        count[sem] = count.get(sem, 0) + 1
+        call(eng[q]).then_inc(T.sem[sem], 1)
+        note(q, sem, count[sem], reads, writes)
+
+    def dma(q, reads, writes, out, in_):
+        order(q, reads, writes)
+        sem = "d%d" % ndma[0]
+        ndma[0] += 1
+        count[sem] = 16
+        eng[q].dma_start(out, in_).then_inc(T.sem[sem], 16)
+        note("dma", sem, 16, reads, writes)
+
+    def lands(sem, n, writes):
+        count[sem] = n
+        note("far", sem, n, [], writes)
+
+    def ap(r):
+        return T[r[0]][:, r[1]:r[2]]
+
+    def ts(out, in0, s1, s2, o0, o1=None):
+        cols = [s for s in (s1, s2) if isinstance(s, tuple)]
+        a1, a2 = [ap(s) if isinstance(s, tuple) else s for s in (s1, s2)]
+        if o1 is None:
+            op("v", [in0] + cols, [out], lambda e: e.tensor_scalar(ap(out), ap(in0), a1, None, o0))
+        else:
+            op("v", [in0] + cols, [out], lambda e: e.tensor_scalar(ap(out), ap(in0), a1, a2, o0, o1))
+
+    def tt(out, in0, in1, o):
+        op("v", [in0, in1], [out], lambda e: e.tensor_tensor(ap(out), ap(in0), ap(in1), o))
+
+    def cp(out, in_):
+        op("v", [in_], [out], lambda e: e.tensor_copy(ap(out), ap(in_)))
+
+    def pick(out, win, off):
+        op("v", [win, off], [out], lambda e: e.tensor_copy(ap(out), ap(win).indirect(ap(off))))
+
+    def pick_less(out, win, off, in1):
+        op("v", [win, off, in1], [out], lambda e: e.tensor_tensor(ap(out), ap(win).indirect(ap(off)), ap(in1), Op.subtract))
+
+    def act(out, in_, f, bias=0.0, scale=1.0):
+        op("a", [in_], [out], lambda e: e.activation(ap(out), ap(in_), f, bias, scale))
+
+    def mm(out, lhsT, rhs, start, stop, step=1):
+        r = T[rhs[0]][:, rhs[1]:rhs[2]:step] if step > 1 else ap(rhs)
+        op("t", [lhsT, rhs], [out], lambda e: e.matmul(ap(out), ap(lhsT), r, start, stop))
+
+    def iota(out, pattern, base, cm, small=True):
+        if small:
+            op("g", [], [out], lambda e: e.iota(ap(out), pattern, base, cm, allow_small_or_imprecise_dtypes=True))
+        else:
+            op("g", [], [out], lambda e: e.iota(ap(out), pattern, base, cm))
+
+    def send(to, out, in_, sem):
+        rid, pid = topo.addr(to, core)
+        es = [e for e in topo.engines(core, to) if e not in fold_es]
+        order("g", [in_], [])
+        g.remote_dma(ap(out), ap(in_), T.sem[sem], T.sem.sent, pid, rid, bits(es))
+        count["sent"] = count.get("sent", 0) + len(es)
+
+    helper = helper_of(core, T, topo)
+    fold_es = fold_engines(core, T, topo)
+    n_far = len(topo.engines(core, helper)) - len(fold_es)
+
+    def Lf(i, h=None):
+        return ("L", 16 * i, 16 * i + 16) if h is None else ("L", 16 * i + 8 * h, 16 * i + 8 * h + 8)
+
+    def col(i, j):
+        return ("L", 16 * i + j, 16 * i + j + 1)
+
+    def Ek(w, k):
+        return (w, 128 - k, 256 - k)
+
+    RW, RGW, XW = ("R", 0, V), ("Rg", 0, V), ("Xs", K, K + V)
+    OC, GC, U, TL, Z1, W1, KEY, ZF, ZM, ZS, DUM, WC, T1, T2, CO, NUM = range(16)
+    IB, NIB, BIB, IF = ("Ib", 0, 128), ("nIb", 0, 128), ("bIb", 0, 128), ("If", 0, 128)
+
+    def turn(t, src, name):
+        a = 16 * t
+        dma("s", [(name, 0, V)], [RGW], T.Rg[0:128 - a, :], src[a:128, 0:V])
+        first = hist.pop("Rg")
+        dma("s", [(name, 0, V)], [RGW], T.Rg[128 - a:128, :], src[0:a, 0:V])
+        hist["Rg"] = first + hist["Rg"]
+
+    dma("s", [], [("w0i", 0, 16)], T.w0i[:, :], T.w0[:, :])
+    dma("s", [], [RW], T.R[:, 0:V], T.rec[:, :])
+    dma("s", [], [("Xs", K - 1, K - 1 + V)], T.Xs[:, K - 1:K - 1 + V], T.x[:, :])
+    turn(1, T.rec, "rec")
+
+    iota(("Li", 0, 4), [[-1, 4]], 16, 1, False)
+    iota(("Li", 4, 5), [[0, 1]], 0, 1, False)
+    iota(("J", 0, 256), [[0, 2], [1, 128]], 0, 0)
+    iota(("Gm", 0, 128), [[16, 8], [0, 16]], 0, 0)
+    iota(("Km", 0, 144), [[0, 9], [1, 16]], 0, 0)
+    iota(("thr", 0, K), [[1, K]], 0, 0)
+    iota(("R", V, 2048), [[0, 256]], 0, 0, False)
+    p_ = ("Li", 4, 5)
+    ts(("Li", 8, 12), ("Li", 0, 4), 15, None, Op.bitwise_and)
+    ts(("Li", 12, 13), p_, 112, None, Op.bitwise_and)
+    ts(("Li", 13, 14), p_, 7, None, Op.bitwise_and)
+    ts(("Li", 14, 15), p_, 3, 1, Op.arith_shift_right, Op.bitwise_and)
+    ts(("Li", 16, 17), p_, 4, 1, Op.arith_shift_right, Op.bitwise_and)
+    ts(("Li", 17, 18), p_, 1, None, Op.bitwise_and)
+    cp(("L", 16 * OC, 16 * OC + 7), ("Li", 8, 15))
+    cp(col(GC, 0), p_)
+    gcol, pcol, kcol, qcol, bcol, odd = col(OC, 4), col(GC, 0), col(OC, 0), col(OC, 5), col(OC, 6), col(GC, 1)
+    tt(odd, ("Li", 16, 17), ("Li", 17, 18), Op.not_equal)
+    ts(col(GC, 2), qcol, 16.0, bcol, Op.mult, Op.add)
+    ts(col(GC, 5), qcol, 0.0, odd, Op.is_equal, Op.mult)
+    ts(col(GC, 3), odd, 240.0, col(GC, 2), Op.mult, Op.add)
+    ts(col(GC, 4), col(GC, 5), 256.0, col(GC, 3), Op.mult, Op.add)
+    ts(("Lu", 8, 16), ("J", 64, 72), 2.0, col(GC, 3), Op.mult, Op.add)
+    ts(("Lu", 0, 8), ("J", 0, 8), 2.0, col(GC, 4), Op.mult, Op.add)
+    ts(IF, ("J", 0, 128), pcol, None, Op.is_equal)
+    ts(("Wb", 0, 256), ("J", 0, 256), gcol, None, Op.is_equal)
+    ts(("Wh", 0, 256), ("J", 0, 256), gcol, None, Op.is_equal)
+    ts(("BDb", 0, 128), ("Gm", 0, 128), gcol, None, Op.is_equal)
+    ts(("BDh", 0, 128), ("Gm", 0, 128), gcol, None, Op.is_equal)
+    ts(Lf(NUM), ("J", 0, 16), 16.0, kcol, Op.mult, Op.add)
+    for t in range(1, RO + 1):
+        ts(("Tq", 0, 128), ("Km", 16 - t, 144 - t), col(OC, t), -BIG, Op.is_gt, Op.mult)
+        tt(("Tri", 128 * (t - 1), 128 * t), ("Tq", 0, 128), ("BDb", 0, 128), Op.mult)
+    for n in sorted(set(NS_OWN[0] + NS_OWN[1] + NS_OWN[2])):
+        ts(col(CO, n), kcol, 4.0 * n, 4.0, Op.is_lt, Op.mult)
+    ts(col(CO, 8), kcol, 4.0 * NS_NEAR, 6.0, Op.is_lt, Op.mult)
+    ts(Lf(DUM), Lf(NUM), float(V + K - 1), None, Op.add)
+    act(IB, IF, Fn.Copy)
+    act(NIB, IF, Fn.Copy, 0.0, -1.0)
+    act(BIB, IF, Fn.Copy, 0.0, BIG)
+    act(("Wl", 0, 256), ("Wb", 0, 256), Fn.Copy, 0.0, 256.0)
+    act(Lf(WC), Lf(NUM), Fn.Exp, 128 * LNB, -LNB)
+    act(("thr", 0, K), ("thr", 0, K), Fn.Exp, 128 * LNB + math.log(2.55), -LNB)
+    cp(("q0", 256, 272), ("w0i", 0, 16))
+    cp(("q0", 272, 273), ("w0i", 0, 1))
+    ts(Lf(W1), ("w0i", 0, 16), float(K), 1.0 / BIG, Op.add, Op.mult)
+
+    late = []
+
+    def run_late(n):
+        for _ in range(min(n, len(late))):
+            late.pop(0)()
+
+    def ch(name, h, c, n=1):
+        return (name, 2048 * h + 512 * c, 2048 * h + 512 * (c + n))
+
+    def row(name, h, k):
+        return (name, 2048 * h + H * k, 2048 * h + H * k + H)
+
+    def hf(name, h, at=0):
+        return (name, at + H * h, at + H * h + H)
+
+    def store(s):
+        dma("s", [("ss", K * s, K * s + K)], [], T.y[:, K * s:K * s + K], T.ss[:, K * s:K * s + K])
+
+    def step(t):
+        s = t - 1
+        last = t == RO
+        q, qn = "q%d" % s, "q%d" % t
+        A = "A%d" % (s % 2)
+        guest, asker = T.cores[(rank + t) % N], T.cores[(rank - t) % N]
+        lq0 = 272 * s
+        ns = NS_OWN[s]
+        CN = [("P", 0, H), ("P", 512, 512 + H)]
+        ZL = [("P", 128, 136), ("P", 640, 648)]
+        KR = [("P", 256, 256 + H), ("P", 768, 768 + H)]
+        CG = [("P", 1024, 1024 + H), ("P", 1152, 1152 + H)]
+        VAL = [("P", 1536, 1536 + H), ("P", 1280, 1280 + H)]
+        NR = [("P", 1664, 1664 + H), ("P", 1792, 1792 + H)]
+        WL = ("P", 144, 160)
+        began = set()
+
+        def PB(c):
+            return ("P", 2048 + 512 * c, 2048 + 512 * c + 512)
+
+        def spread(name, h, src=None):
+            a = 512 * h
+            if src is not None:
+                act((name, a, a + H), src, Fn.Copy)
+            act((name, a + H, a + 2 * H), src or (name, a, a + H), Fn.Copy)
+            act((name, a + 2 * H, a + 4 * H), (name, a, a + 2 * H), Fn.Copy)
+
+        def own_pick(h, c):
+            o = 128 * h + 32 * c
+            pick_less(ch("dO", h, c), RW, (q, o, o + 32), ("R4", 512 * h, 512 * h + 512))
+
+        def guest_pick(h, c):
+            o = lq0 + 128 * h + 32 * c
+            pick_less(ch("dG", h, c), RGW, ("lq", o, o + 32), ("G4", 512 * h, 512 * h + 512))
+
+        def test_v(d, h, c, n):
+            if n > 0:
+                ts(ch(d, h, c, n), ch(d, h, c, n), C4, C4, Op.add, Op.is_equal)
+
+        def test_s(h, c, n):
+            if n > 0:
+                act(ch("dO", h, c, n), ch("dO", h, c, n), Fn.Abs)
+                act(ch("dO", h, c, n), ch("dO", h, c, n), Fn.Sign, 2.5, -1.0)
+
+        def tally(out, d, h, c, n, total):
+            for k in range(4 * c, 4 * (c + n)):
+                m = len([1 for b in began if b[0] == out])
+                began.add((out, k))
+                mm(out, Ek("Wb", k), row(d, h, k), m == 0, m + 1 == total)
+
+        def guest_half(h):
+            for c in range(3):
+                guest_pick(h, c)
+            test_v("dG", h, 0, 2)
+            tally(CG[h], "dG", h, 0, 2, 16)
+            guest_pick(h, 3)
+            for c in (2, 3):
+                test_v("dG", h, c, 1)
+                tally(CG[h], "dG", h, c, 1, 16)
+
+        def answer(h):
+            act(hf("an", h, K * s), CG[h], Fn.Sign, -11.5)
+            send(asker, hf("la", h, K * s), hf("an", h, K * s), "aa%d" % (2 * s + h))
+
+        def x_pick(h, c, n=1):
+            out, o = ch("XC", h, c, n), 128 * h + 32 * c
+            off = (q, o, o + 32 * n)
+            op("a", [XW, off], [out], lambda e: e.activation(ap(out), ap(XW).indirect(ap(off)), Fn.Copy))
+
+        def x_load(h, c):
+            mm(PB(c), IB, ch("XC", h, c), True, False)
+
+        def x_less(h, c):
+            b = PB(c)[1]
+            for i in range(4):
+                mm(("P", b + H * i, b + H * i + H), NIB, hf("xz", h), False, i == 3)
+
+        def x_abs(h, c):
+            act(ch(A, h, c), PB(c), Fn.Abs)
+
+        def near_s(h, c, n=1):
+            act(ch("dO", h, c, n), ch(A, h, c, n), Fn.Sign, 0.5 + 2.0 ** -20, -1.0)
+
+        def near_v(h, c):
+            ts(ch("dO", h, c), PB(c), C1, C1, Op.add, Op.is_equal)
+
+        def twin(h):
+            mm(CN[h], BIB, hf("la", h, K * s), False, True)
+            ts(hf("twin", h), CN[h], col(CO, ns[h]), BIG + 11.5, Op.add, Op.is_ge)
+            mm(VAL[h], BIB, hf("twin", h), False, False)
+            mm(VAL[h], ("Tri", 128 * s, 128 * s + 128), hf("twin", h), False, True)
+
+        def choose(h):
+            ts(hf("sel", h), VAL[h], K - BIG, 0.0, Op.add, Op.max)
+            for r in range(16):
+                mm(ZL[h], Ek("Wh", r), ("sel", H * h + r, H * h + H), r == 0, r == 15, 16)
+            if not last:
+                mm(KR[h], ("BDh", 0, 128), hf("sel", h), True, True)
+
+        def after(h):
+            j16 = ("Lu", 16 + 8 * h, 24 + 8 * h)
+            tt(Lf(T2, h), ZL[h], Lf(NUM, h), Op.max)
+            cp(j16, Lf(T2, h))
+            pick(hf("xz", h), ("Xs", 0, K + V), j16)
+
+        def keys(h):
+            cp(Lf(KEY, h), ZL[h])
+            cp(hf("key", h), KR[h])
+            ts(Lf(U, h), Lf(KEY, h), 0.0, BIG, Op.is_equal, Op.mult)
+
+        at = [0]
+
+        def claims(h, b0, b1):
+            for b in range(b0, b1):
+                lo = max(16 * b, H * h)
+                n = H * h + H - lo
+                e = ("dG", at[0], at[0] + n)
+                at[0] += n
+                ts(e, ("key", lo, lo + n), col(KEY, b), col(WC, b), Op.is_equal, Op.mult)
+                mm(("P", CN[h][2] - n, CN[h][2]), ("BDb", 0, 128), e, b == 0, b == 8 * h + 7)
+
+        def loses(h):
+            tt(hf("win", h), CN[h], hf("thr", h), Op.is_ge)
+
+        def listed():
+            mm(WL, IF, Lf(ZS), True, False)
+            for r in range(16):
+                mm(WL, Ek("Wl", r), ("win", r, K), False, r == 15, 16)
+
+        def place(i, h):
+            if i == 0:
+                tt(Lf(TL, h), Lf(U, h), Lf(W1, h), Op.mult)
+            if i == 1:
+                tt(Lf(Z1, h), Lf(KEY, h), Lf(TL, h), Op.add)
+            if i == 2:
+                ts(Lf(ZM, h), Lf(Z1, h), float(V + K - 1), -float(V), Op.is_ge, Op.mult)
+            if i == 3:
+                tt(Lf(ZF, h), Lf(ZM, h), Lf(Z1, h), Op.add)
+            if i == 4:
+                ts((qn, 256 + 8 * h, 264 + 8 * h), Lf(ZF, h), 1.0 - K, None, Op.add)
+                tt(Lf(ZS, h), Lf(ZF, h), Lf(U, h), Op.add)
+                ts(Lf(W1, h), Lf(ZF, h), 1.0, 1.0 / BIG, Op.add, Op.mult)
+                if h == 0:
+                    ts((qn, 272, 273), col(ZF, 0), 1.0 - K, None, Op.add)
+
+        def old(h):
+            pick_less(hf("dl", h), RW, (qn, 256 + 8 * h, 264 + 8 * h), hf("nn", h))
+
+        def target(i):
+            if i == 0:
+                tt(Lf(T1), WL, Lf(DUM), Op.min)
+            if i == 1:
+                ts(("Lu", 32, 48), Lf(T1), 1.0 - K, None, Op.add)
+
+        def write(h):
+            off = ("Lu", 32 + 8 * h, 40 + 8 * h)
+            op("v", [hf("nw", h), off], [("R", 0, 2048)], lambda e: e.tensor_copy(T.R[:, :].indirect(ap(off)), ap(hf("nw", h))))
+
+        def put(i, h):
+            if i == 0 and h == 0:
+                ts(NR[h], NR[h], 3.0, None, Op.is_lt)
+            if i == 0 and h == 1:
+                ts(NR[h], NR[h], col(CO, 8), 9.5, Op.add, Op.is_lt)
+            if i == 1:
+                tt(NR[h], NR[h], hf("dl", h), Op.mult)
+            if i == 2:
+                tt(hf("nw", h), NR[h], hf("nn", h), Op.add)
+
+        def expo(h, c, n):
+            act(ch(A, h, c, n), ch(A, h, c, n), Fn.Exp, 0.0, -1.0)
+
+        def fold():
+            rid, pid = topo.addr(helper, core)
+            order("g", [(A, 0, 4096)], [])
+            n = len(fold_es) // 2
+            trs = [RemoteDMATransfer(dst_ids=[DstId(rid=rid, pnc=pid)], dma_engine_mask=bits(fold_es[n * h:n * h + n]),
+                                     remote_sem=T.sem["hin%d" % s], srcs=[ap(row(A, h, k)) for k in range(16)],
+                                     dsts=[ap(hf("ss", h, K * s))], alu_op=1) for h in (0, 1)]
+            g.remote_dma_fused(trs, local_sem=T.sem["fold%d" % s])
+            count["fold%d" % s] = len(fold_es)
+            note("far", "fold%d" % s, len(fold_es), [(A, 0, 4096)], [])
+            lands("back%d" % s, len(topo.engines(helper, core)), [("ss", K * s, K * s + K)])
+
+        pick(("Rw", 0, 272), RW, (q, 256, 273))
+        op("v", [("Rw", 0, 256)], [("Tr", 0, 256)], lambda e: e.transpose(T.Tr[:, 0:256], T.Rw[:, 0:256]))
+        op("v", [("Rw", 16, 272)], [("Tr", 256, 512)], lambda e: e.transpose(T.Tr[:, 256:512], T.Rw[:, 16:272]))
+        spread("R4", 0, hf("Rw", 0))
+        pick((q, 0, 256), ("Tr", 0, 512), ("Lu", 0, 16))
+        send(guest, ("lq", lq0, lq0 + 272), (q, 0, 272), "qa%d" % s)
+        lands("qa%d" % s, n_far, [("lq", lq0, lq0 + 272)])
+        for h in (0, 1):
+            lands("aa%d" % (2 * s + h), n_far, [hf("la", h, K * s)])
+        if not last:
+            act(("rr", 0, K), ("Rw", 0, K), Fn.Relu, -float(V * (V - 2)), float(V))
+            mm(("P", 1024, 1280), IF, ("Rw", 0, K), True, False)
+            mm(("P", 1024, 1280), NIB, ("rr", 0, K), False, True)
+        mm(VAL[0], IF, hf("Rw", 0), True, False)
+        spread("R4", 1, hf("Rw", 1))
+        if not last:
+            act(("nn", 0, K), ("P", 1024, 1280), Fn.Identity, 1.0)
+        if t == 1:
+            act(("Xs", K - 1 + V, K + V), ("Xs", K - 1, K), Fn.Copy)
+        run_late(99)
+        for c in range(4):
+            own_pick(0, c)
+        if EARLY:
+            own_pick(1, 0)
+        if t == 1:
+            test_s(0, 0, ns[0])
+        else:
+            x_pick(0, 0)
+        for h in (0, 1):
+            pick(("G4", 512 * h, 512 * h + H), RGW, ("lq", lq0 + 256 + 8 * h, lq0 + 264 + 8 * h))
+            if h == 0:
+                spread("G4", 0)
+        test_v("dO", 0, ns[0], 4 - ns[0])
+        tally(CN[0], "dO", 0, ns[0], 4 - ns[0], 99)
+        spread("G4", 1)
+        if t == 1:
+            x_pick(0, 0, 2); x_pick(0, 2, 2)
+        else:
+            test_s(0, 0, ns[0])
+            x_pick(0, 1)
+        guest_half(0)
+        answer(0)
+        tally(CN[0], "dO", 0, 0, ns[0], 99)
+        if t > 1:
+            x_pick(0, 2, 2)
+        op("a", [XW, (q, 256, 272)], [("Xs", 0, K)],
+           lambda e: e.activation(T.Xs[:, 0:K], ap(XW).indirect(ap((q, 256, 272))), Fn.Copy))
+        x_pick(1, 0, 2)
+        if t == 1:
+            x_pick(1, 2)
+        for c in range(4):
+            x_load(0, c)
+        guest_half(1)
+        answer(1)
+        if last:
+            store(s - 1)
+        twin(0)
+        mm(VAL[1], IF, hf("Rw", 1), True, False)
+        early = EARLY
+        own_pick(1, early)
+        if t > 1:
+            x_pick(1, 2)
+        test_s(1, 0, ns[1])
+        x_pick(1, 3)
+        choose(0)
+        own_pick(1, early + 1)
+        after(0)
+        for c in range(4):
+            x_less(0, c)
+            x_abs(0, c)
+            if c == 1 and not last:
+                near_s(0, 0, 2)
+        if not last:
+            keys(0)
+        if not early:
+            own_pick(1, 2)
+        tally(CN[1], "dO", 1, 0, ns[1], 99)
+        test_v("dO", 1, ns[1], 2 + early - ns[1])
+        tally(CN[1], "dO", 1, ns[1], 2 + early - ns[1], 99)
+        if not early:
+            x_load(1, 0); x_load(1, 1)
+        own_pick(1, 3)
+        for c in range(2 + early, 4):
+            test_v("dO", 1, c, 1)
+            tally(CN[1], "dO", 1, c, 1, 99)
+        if not last:
+            near_s(0, 2, 2)
+            place(0, 0)
+            claims(0, 0, 2)
+            place(1, 0)
+            claims(0, 2, 4)
+            place(2, 0)
+            twin(1)
+            if early:
+                x_load(1, 0); x_load(1, 1)
+            else:
+                tally(NR[0], "dO", 0, 0, 2, 16)
+            place(3, 0)
+            claims(0, 4, 8)
+            place(4, 0)
+            choose(1)
+            if early:
+                tally(NR[0], "dO", 0, 0, 2, 16)
+            x_load(1, 2); x_load(1, 3)
+            old(0)
+            loses(0)
+            after(1)
+            for c in (0, 1, 3, 2):
+                x_less(1, c)
+            keys(1)
+            x_abs(1, 0)
+            for c in range(NS_NEAR):
+                if c + 1 < NS_NEAR:
+                    x_abs(1, c + 1)
+                near_s(1, c)
+            tally(NR[0], "dO", 0, 2, 2, 16)
+            for i in range(4):
+                claims(1, 2 * i, 2 * i + 2)
+                place(i, 1)
+            claims(1, 8, 16)
+            place(4, 1)
+            put(0, 0)
+            for c in range(NS_NEAR, 4):
+                near_v(1, c)
+            put(1, 0)
+            loses(1)
+            listed()
+            put(2, 0)
+            old(1)
+            tally(NR[1], "dO", 1, 0, min(2, NS_NEAR), 16)
+            tally(NR[1], "dO", 1, NS_NEAR, 4 - NS_NEAR, 16)
+            tally(NR[1], "dO", 1, 2, NS_NEAR - 2, 16)
+            target(0); target(1)
+            write(0)
+            put(0, 1); put(1, 1); put(2, 1)
+            write(1)
+            turn(t + 1, T.R, "R")
+            if s > 0:
+                store(s - 1)
+            for c in range(NS_NEAR, 4):
+                x_abs(1, c)
+            expo(0, 0, 2); expo(0, 2, 2)
+            late.extend([lambda: expo(1, 0, 2), lambda: expo(1, 2, 2), fold])
+        else:
+            expo(0, 0, 2); expo(0, 2, 2)
+            twin(1)
+            if early:
+                x_load(1, 0); x_load(1, 1)
+            choose(1)
+            x_load(1, 2); x_load(1, 3)
+            for k in range(2):
+                mm(CN[0], IF, row(A, 0, k), k == 0, k == 15)
+            after(1)
+            for c in (0, 3, 1, 2):
+                x_less(1, c)
+            for k in range(2, 16):
+                mm(CN[0], IF, row(A, 0, k), k == 0, k == 15)
+            ts(("acc", 512, 1024), PB(3), -1.0, None, Op.mult)
+            tt(ch(A, 1, 3), PB(3), ("acc", 512, 1024), Op.max)
+            for i, c in enumerate((0, 3, 1, 2)):
+                if c != 3:
+                    x_abs(1, c)
+                a, b = ch(A, 1, c)[1], PB(c)[1]
+                if i == 0:
+                    act(("acc", 0, K), (A, a, a + K), Fn.Exp, 0.0, -1.0)
+                    act(("P", b, b + K), (A, a + K, a + 2 * K), Fn.Exp, 0.0, -1.0)
+                    tt(("acc", 0, K), ("P", b, b + K), ("acc", 0, K), Op.add)
+                elif i < 3:
+                    act(PB(c), ch(A, 1, c), Fn.Exp, 0.0, -1.0)
+                    tt(("acc", 0, K), ("P", b, b + K), ("acc", 0, K), Op.add)
+                    tt(("acc", 0, K), ("P", b + K, b + 2 * K), ("acc", 0, K), Op.add)
+                else:
+                    b2 = PB(0)[1]
+                    act(("P", b, b + K), (A, a, a + K), Fn.Exp, 0.0, -1.0)
+                    act(("P", b2, b2 + K), (A, a + K, a + 2 * K), Fn.Exp, 0.0, -1.0)
+                    tt(("acc", 0, K), ("P", b, b + K), ("acc", 0, K), Op.add)
+                    cp(hf("yo", 0), CN[0])
+                    tt(("acc", 0, K), ("P", b2, b2 + K), ("acc", 0, K), Op.add)
+            tt(hf("yo", 1), ("acc", 0, H), ("acc", H, K), Op.add)
+            dma("s", [("yo", 0, K)], [], T.y[:, K * s:K * s + K], T.yo[:, :])
+
+    for t in range(1, RO + 1):
+        step(t)
+    for sem, n in count.items():
+        need("s", sem, n, {})

@@ -3,39 +3,47 @@ from concourse.bass import DstId, RemoteDMATransfer
 from concourse.mybir import AluOpType as Op, ActivationFunctionType as Fn
 
 V, K, RO, H = 1792, 256, 3, 128
+F, S = 1, 0
 BIG = 4096.0
+LOW = 2048.0
 C4 = 1.5 * 2.0 ** 25
 C1 = 1.5 * 2.0 ** 23
 LNB = 0.5 * math.log(3.0)
-NS_OWN = ((2, 1), (2, 1), (2, 1))
-EARLY = 1
-NS_NEAR = 3
+OPT = {"ns_own": ((0, 0), (0, 2), (0, 2)), "ns_guest": ((3, 3), (1, 3), (1, 3)), "near": (1, 4), "narrow": 0,
+       "spread": "vvgvg", "shift": {}, "twin": "va", "xz": "va", "slack": 0.07, "rounds": 0, "gnarrow": 0, "hold": 9.0, "gap": 0.5}
+CYCLE, PE, GATHER, SCATTER, WAKE, NEAR, FAR, FIRST, FOLD = 0.00083, 0.0005, 1.6, 3.0, 0.09, 1.3, 1.9, 2.0, 12.0
+TABLE, ISSUE = 6.0, 1.0
+PLAN = {}
 
 SCRATCH = {
-    "R": ("sbuf", [128, 2048], "int32"), "Rg": ("sbuf", [128, V], "int32"), "Xs": ("sbuf", [128, 2048], "bfloat16"),
-    "w0i": ("sbuf", [128, 16], "int32"),
-    "q0": ("sbuf", [128, 288], "uint16"), "q1": ("sbuf", [128, 288], "uint16"), "q2": ("sbuf", [128, 288], "uint16"),
+    "Rh": ("sbuf", [128, 2 * V], "float16"), "Gh": ("sbuf", [128, 2 * V], "float16"),
+    "G2": ("sbuf", [128, 2048], "float32"), "G3": ("sbuf", [128, 2048], "float32"), "up": ("sbuf", [128, 544], "float32"),
+    "lu": ("sbuf", [128, 544], "float32"), "R": ("sbuf", [128, 2048], "int32"), "qh": ("sbuf", [128, 272], "float16"), "qs": ("sbuf", [128, 3 * 272], "uint16"),
+    "Xs": ("sbuf", [128, V + 16], "bfloat16"), "X0": ("sbuf", [128, V], "bfloat16"), "w0i": ("sbuf", [128, 16], "int32"),
+    "q0": ("sbuf", [128, 272], "uint16"), "q1": ("sbuf", [128, 272], "uint16"), "q2": ("sbuf", [128, 272], "uint16"),
+    "q3": ("sbuf", [128, 272], "uint16"), "w0g": ("sbuf", [128, 32], "int32"),
     "lq": ("sbuf", [128, 3 * 272], "uint16"), "an": ("sbuf", [128, 768], "bfloat16"), "la": ("sbuf", [128, 768], "bfloat16"),
-    "Rw": ("sbuf", [128, 272], "float32"), "R4": ("sbuf", [128, 1024], "float32"), "G4": ("sbuf", [128, 1024], "float32"),
-    "Tr": ("sbuf", [128, 512], "float32"),
+    "Rw": ("sbuf", [128, 288], "float32"), "R4": ("sbuf", [128, 1024], "float16"), "G4": ("sbuf", [128, 1024], "float16"),
+    "Tr": ("sbuf", [128, 544], "float32"),
     "dO": ("sbuf", [128, 4096], "bfloat16"), "dG": ("sbuf", [128, 4096], "bfloat16"), "XC": ("sbuf", [128, 4096], "bfloat16"),
+    "gh": ("sbuf", [128, 2048], "float16"), "nr": ("sbuf", [128, 4096], "bfloat16"), "eq": ("sbuf", [128, 1152], "bfloat16"),
     "A0": ("sbuf", [128, 4096], "float32"), "A1": ("sbuf", [128, 4096], "float32"),
     "twin": ("sbuf", [128, K], "bfloat16"), "sel": ("sbuf", [128, K], "float16"), "key": ("sbuf", [128, K], "float16"),
-    "xz": ("sbuf", [128, K], "bfloat16"), "rr": ("sbuf", [128, K], "bfloat16"), "nn": ("sbuf", [128, K], "float32"),
-    "dl": ("sbuf", [128, K], "float32"), "nw": ("sbuf", [128, K], "float32"),
-    "win": ("sbuf", [128, K], "bfloat16"), "thr": ("sbuf", [128, K], "float32"),
-    "L": ("sbuf", [128, 256], "float32"), "Li": ("sbuf", [128, 32], "int32"), "Lu": ("sbuf", [128, 64], "uint16"),
+    "xz": ("sbuf", [128, K], "bfloat16"), "rr": ("sbuf", [128, K], "bfloat16"), "nn": ("sbuf", [128, K], "float16"),
+    "dl": ("sbuf", [128, K], "float32"),
+    "win": ("sbuf", [128, K], "bfloat16"), "thf": ("sbuf", [128, H], "float32"), "thr": ("sbuf", [128, H], "bfloat16"),
+    "L": ("sbuf", [128, 192], "float32"), "Li": ("sbuf", [128, 64], "int32"), "Lu": ("sbuf", [128, 48], "uint16"),
     "ss": ("sbuf", [128, 512], "float32"), "acc": ("sbuf", [128, 1024], "float32"), "yo": ("sbuf", [128, K], "float32"),
-    "J": ("sbuf", [128, 256], "float32"), "Km": ("sbuf", [128, 144], "float32"), "Gm": ("sbuf", [128, 128], "float32"),
-    "Wb": ("sbuf", [128, 256], "bfloat16"), "Wh": ("sbuf", [128, 256], "float16"), "Wl": ("sbuf", [128, 256], "bfloat16"),
-    "BDb": ("sbuf", [128, 128], "bfloat16"), "BDh": ("sbuf", [128, 128], "float16"),
-    "Ib": ("sbuf", [128, 128], "bfloat16"), "nIb": ("sbuf", [128, 128], "bfloat16"), "bIb": ("sbuf", [128, 128], "bfloat16"),
-    "If": ("sbuf", [128, 128], "float32"), "Tri": ("sbuf", [128, 384], "bfloat16"), "Tq": ("sbuf", [128, 128], "bfloat16"),
+    "J": ("sbuf", [128, 128], "float32"), "Km": ("sbuf", [128, 144], "bfloat16"), "Gm": ("sbuf", [128, 128], "bfloat16"),
+    "Wb": ("sbuf", [128, 320], "bfloat16"), "Wl": ("sbuf", [128, 256], "bfloat16"), "BD": ("sbuf", [128, 128], "bfloat16"),
+    "Ib": ("sbuf", [128, 256], "bfloat16"), "nIb": ("sbuf", [128, 128], "bfloat16"), "bIb": ("sbuf", [128, 128], "bfloat16"),
+    "If": ("sbuf", [128, 128], "float32"), "Tri": ("sbuf", [128, 384], "bfloat16"), "Tq": ("sbuf", [128, 384], "bfloat16"),
     "P": ("psum", [128, 4096], "float32"),
 }
 NDMA = 16
-SEMAPHORES = (["sv", "sa", "st", "sg", "sent", "fold0", "fold1", "hin0", "hin1", "back0", "back1"]
-              + ["qa%d" % i for i in range(RO)] + ["aa%d" % i for i in range(2 * RO)] + ["d%d" % i for i in range(NDMA)])
+SEMAPHORES = (["sv", "sa", "st", "sg", "sent", "ta0", "qa0", "aa0", "aa1", "up1", "up2"]
+              + ["%s%d" % (n, t) for n in ("tin", "tb") for t in (2, 3)]
+              + [n + str(i) for n in ("fold", "hin", "back") for i in range(4)] + ["d%d" % i for i in range(NDMA)])
 
 
 def helper_of(core, T, topo):
@@ -43,6 +51,30 @@ def helper_of(core, T, topo):
         if c != core and T.rank_of(c) is None and topo.die(c) == topo.die(core):
             return c
     return None
+
+
+def asker_of(core, t, T):
+    return T.cores[(T.rank_of(core) - t) % len(T.cores)]
+
+
+def relay_of(core, T, topo):
+    for c in topo.cores_of(core):
+        if (T.rank_of(c) is None and topo.die(c) == topo.die(core) and c != helper_of(core, T, topo)
+                and all(topo.may_write(c, asker_of(core, t, T)) for t in (2, 3))):
+            return c
+    return None
+
+
+def hand_on(g, core, owner, T, topo):
+    near = fold_engines(owner, T, topo)
+    for t in (2, 3):
+        to = asker_of(owner, t, T)
+        rid, pid = topo.addr(to, core)
+        es = [e for e in topo.engines(core, to) if e not in near]
+        g.wait_ge(T.sem["tin%d" % t], len(near))
+        lists = T.Gh[:, V * (t - 2):V * (t - 1)]
+        g.remote_dma(lists, lists, T.sem["tb%d" % t], T.sem.sent, pid, rid, bits(es))
+    g.wait_ge(T.sem.sent, 2 * len(es))
 
 
 def bits(engines):
@@ -58,8 +90,13 @@ def rank_program(g, core, T, topo):
         for c in T.cores:
             if helper_of(c, T, topo) == core:
                 hand_back(g, core, c, T, topo)
+            if relay_of(c, T, topo) == core:
+                hand_on(g, core, c, T, topo)
         return
-    walk(g, core, rank, T, topo)
+    jobs = walk(g, core, rank, T, topo)
+    if "order" not in PLAN:
+        PLAN["order"] = arrange(jobs)
+    issue(g, T, [jobs[i] for i in PLAN["order"]])
 
 
 def fold_engines(core, T, topo):
@@ -71,20 +108,101 @@ def hand_back(g, core, owner, T, topo):
     rid, pid = topo.addr(owner, core)
     n = len(fold_engines(owner, T, topo))
     m = topo.mask(core, owner)
-    for s in range(RO - 1):
-        g.wait_ge(T.sem["hin%d" % s], n)
-        g.remote_dma(T.ss[:, s * K:(s + 1) * K], T.ss[:, s * K:(s + 1) * K], T.sem["back%d" % s], T.sem.sent, pid, rid, m)
-    g.wait_ge(T.sem.sent, (RO - 1) * len(topo.engines(core, owner)))
+    for i in [2 * s + h for s in range(RO - 1) for h in (F, S)]:
+        g.wait_ge(T.sem["hin%d" % i], n)
+        half = T.ss[:, i * H:i * H + H]
+        g.remote_dma(half, half, T.sem["back%d" % i], T.sem.sent, pid, rid, m)
+    g.wait_ge(T.sem.sent, 2 * (RO - 1) * len(topo.engines(core, owner)))
 
 
-def walk(g, core, rank, T, topo):
-    N = len(T.cores)
+def earlier(hist, q, reads, writes, plan):
+    found = []
+    for rs, w in ((reads, False), (writes, True)):
+        for name, lo, hi in rs:
+            for lo2, hi2, w2, q2, mark in hist.get(name, []):
+                if name == "P" and (q2 != q or q == "t"):
+                    hit = (plan or q2 != q) and lo // 512 <= (hi2 - 1) // 512 and lo2 // 512 <= (hi - 1) // 512
+                else:
+                    hit = lo < hi2 and lo2 < hi and (w or w2)
+                if hit:
+                    found.append(mark)
+    return found
+
+
+def remember(hist, q, reads, writes, mark):
+    for rs, w in ((reads, False), (writes, True)):
+        for name, lo, hi in rs:
+            h = hist.setdefault(name, [])
+            if w:
+                h[:] = [e for e in h if not (lo <= e[0] and e[1] <= hi and (name != "P" or e[3] == q))]
+            h.append((lo, hi, w, q, mark))
+
+
+def arrange(jobs):
+    hist, deps = {}, []
+    for i, j in enumerate(jobs):
+        deps.append(set(earlier(hist, j["q"], j["reads"], j["writes"], True)))
+        remember(hist, j["q"], j["reads"], j["writes"], i)
+    behind = {(p, i) for i, j in enumerate(jobs) for p in j["behind"] if p not in deps[i]}
+    for p, i in behind:
+        deps[i].add(p)
+    users = [[] for _ in jobs]
+    for i, d in enumerate(deps):
+        for p in d:
+            users[p].append(i)
+
+    def gap(p, i):
+        if (p, i) in behind:
+            return 0.0
+        return jobs[p]["late"] + (0.0 if jobs[p]["q"] == jobs[i]["q"] == "t" else WAKE)
+
+    def run(before, after, urgency, wait, forward, timed=True):
+        left = [len(d) for d in before]
+        ready = {i: 0.0 if forward else jobs[i]["late"] for i in range(len(jobs)) if not before[i]}
+        free, done, order = {}, [0.0] * len(jobs), []
+        due, lag = {}, 0.0
+        if timed:
+            for i in sorted(range(len(jobs)), key=lambda i: urgency[i]):
+                due.setdefault(jobs[i]["q"], []).append(i)
+            top = max(urgency)
+
+        def in_the_way(c, at):
+            u = due[jobs[c]["q"]][-1]
+            return u != c and top - urgency[u] + lag < at + jobs[c]["cost"] - OPT["hold"] and urgency[u] > urgency[c] + OPT["gap"]
+
+        while ready:
+            start = {i: max(r, free.get(jobs[i]["q"], 0.0)) for i, r in ready.items()}
+            able = [i for i in ready if not timed or not in_the_way(i, start[i])] or list(ready)
+            first = min(able, key=lambda i: (start[i], -urgency[i], i))
+            q = jobs[first]["q"]
+            i = max([c for c in able if jobs[c]["q"] == q and start[c] <= start[first] + OPT["slack"]],
+                    key=lambda c: (urgency[c], -c))
+            done[i] = free[q] = start[i] + jobs[i]["cost"]
+            if timed:
+                due[q].remove(i)
+                lag = max(lag, start[i] - top + urgency[i])
+            order.append(i)
+            del ready[i]
+            for u in after[i]:
+                left[u] -= 1
+                if left[u] == 0:
+                    ready[u] = max([done[p] + wait(p, u) for p in before[u]] + [0.0 if forward else jobs[u]["late"]])
+        return max(d + (j["late"] if forward else 0.0) for d, j in zip(done, jobs)), order, done
+
+    best = run(deps, users, [OPT["shift"].get(j["tag"], 0) - i for i, j in enumerate(jobs)], gap, True, False)
+    last = best
+    for _ in range(OPT["rounds"]):
+        back = run(users, deps, last[2], lambda p, u: gap(u, p), False)
+        last = run(deps, users, back[2], gap, True)
+        best = min(best, last)
+    return best[1]
+
+
+def issue(g, T, jobs):
     eng = {"v": g.vector, "a": g.scalar, "t": g.tensor, "g": g, "s": g.sync}
-    own = {"v": "sv", "a": "sa", "t": "st", "g": "sg"}
     count = {}
     known = {q: {} for q in eng}
     hist = {}
-    ndma = [0]
 
     def need(q, sem, val, kn):
         if known[q].get(sem, 0) >= val:
@@ -95,95 +213,130 @@ def walk(g, core, rank, T, topo):
             if known[q].get(s, 0) < n:
                 known[q][s] = n
 
-    def order(q, reads, writes):
-        deps = []
-        for rs, w in ((reads, False), (writes, True)):
-            for name, lo, hi in rs:
-                for lo2, hi2, w2, q2, sem, val, kn in hist.get(name, []):
-                    if name == "P":
-                        if q2 != q:
-                            hit = lo // 512 <= (hi2 - 1) // 512 and lo2 // 512 <= (hi - 1) // 512
-                        else:
-                            hit = q != "t" and lo < hi2 and lo2 < hi and (w or w2)
-                    else:
-                        hit = lo < hi2 and lo2 < hi and (w or w2)
-                    if hit:
-                        deps.append((val, sem, kn))
-        deps.sort(key=lambda d: -d[0])
-        for val, sem, kn in deps:
-            need(q, sem, val, kn)
+    for j in jobs:
+        q, sem = j["q"], j["sem"]
+        if q in eng:
+            for val, s, kn in sorted(earlier(hist, q, j["reads"], j["writes"], False), key=lambda d: -d[0]):
+                need(q, s, val, kn)
+            made = j["call"](eng[q])
+            if not j["remote"]:
+                made.then_inc(T.sem[sem], j["inc"])
+        count[sem] = count.get(sem, 0) + j["inc"]
+        mine = [r for r in j["writes"] if r[0] != "far"]
+        if sem != "sent":
+            remember(hist, q, [r for r in j["reads"] if r[0] != "far"], mine, (count[sem], sem, dict(known.get(q, {}))))
+    for sem, n in count.items():
+        need("s", sem, n, {})
 
-    def note(q, sem, val, reads, writes):
-        kn = dict(known[q]) if q in known else {}
-        for rs, w in ((reads, False), (writes, True)):
-            for name, lo, hi in rs:
-                h = hist.setdefault(name, [])
-                if w:
-                    h[:] = [e for e in h if not (lo <= e[0] and e[1] <= hi and (name != "P" or e[3] == q))]
-                h.append((lo, hi, w, q, sem, val, kn))
 
-    def op(q, reads, writes, call):
-        order(q, reads, writes)
-        sem = own[q]
-        count[sem] = count.get(sem, 0) + 1
-        call(eng[q]).then_inc(T.sem[sem], 1)
-        note(q, sem, count[sem], reads, writes)
+def walk(g, core, rank, T, topo):
+    N = len(T.cores)
+    jobs = []
+    ndma = [0]
+    held, now = {}, [0]
+    late, early, turn = [], [], [0]
 
-    def dma(q, reads, writes, out, in_):
-        order(q, reads, writes)
-        sem = "d%d" % ndma[0]
+    def job(q, reads, writes, call, cost, sem, inc, late=0.0, remote=False):
+        jobs.append({"q": q, "reads": reads, "writes": writes, "call": call, "cost": cost, "sem": sem, "inc": inc,
+                     "late": late, "remote": remote, "behind": held.get(q, [])[-1:],
+                     "tag": (now[0], q, writes[0][0], reads[0][0] if q != "t" else reads[1][0],
+                             (writes[0] if q != "t" else reads[1])[1] * 2 // SCRATCH[(writes[0] if q != "t" else reads[1])[0]][1][1])
+                     if q in "vat" and reads else None})
+        if q == "g":
+            held[q] = [len(jobs) - 1]
+
+    def behind(q, calls):
+        held[q] = [max(i for i, j in enumerate(jobs) if j["q"] == q)]
+        calls()
+        del held[q]
+
+    def op(q, reads, writes, call, cost):
+        job(q, reads, writes, call, cost, "s" + q, 1)
+
+    def width(r):
+        return 4 if SCRATCH[r[0]][2] in ("float32", "int32") else 2
+
+    def size(r):
+        return r[2] - r[1]
+
+    def dma(reads, writes, out, in_, took):
+        job("s", reads, writes, lambda e: e.dma_start(out, in_), 0.05, "d%d" % ndma[0], 16, NEAR + took)
         ndma[0] += 1
-        count[sem] = 16
-        eng[q].dma_start(out, in_).then_inc(T.sem[sem], 16)
-        note("dma", sem, 16, reads, writes)
 
     def lands(sem, n, writes):
-        count[sem] = n
-        note("far", sem, n, [], writes)
+        job("far" + sem, [("far", len(far), len(far) + 1)], writes, None, 0.001, sem, n)
+        far.append(sem)
 
     def ap(r):
         return T[r[0]][:, r[1]:r[2]]
+
+    def plain(out, in_):
+        return 0.03 + max(64, size(out) * (0.5 if width(out) == width(in_) == 2 else 1)) * CYCLE
 
     def ts(out, in0, s1, s2, o0, o1=None):
         cols = [s for s in (s1, s2) if isinstance(s, tuple)]
         a1, a2 = [ap(s) if isinstance(s, tuple) else s for s in (s1, s2)]
         if o1 is None:
-            op("v", [in0] + cols, [out], lambda e: e.tensor_scalar(ap(out), ap(in0), a1, None, o0))
+            op("v", [in0] + cols, [out], lambda e: e.tensor_scalar(ap(out), ap(in0), a1, None, o0), plain(out, in0))
         else:
-            op("v", [in0] + cols, [out], lambda e: e.tensor_scalar(ap(out), ap(in0), a1, a2, o0, o1))
+            op("v", [in0] + cols, [out], lambda e: e.tensor_scalar(ap(out), ap(in0), a1, a2, o0, o1), plain(out, in0))
 
     def tt(out, in0, in1, o):
-        op("v", [in0, in1], [out], lambda e: e.tensor_tensor(ap(out), ap(in0), ap(in1), o))
+        op("v", [in0, in1], [out], lambda e: e.tensor_tensor(ap(out), ap(in0), ap(in1), o),
+           0.03 + max(64, size(out) * (1 if "P" in (in0[0], in1[0]) else 2)) * CYCLE)
 
     def cp(out, in_):
-        op("v", [in_], [out], lambda e: e.tensor_copy(ap(out), ap(in_)))
+        op("v", [in_], [out], lambda e: e.tensor_copy(ap(out), ap(in_)), plain(out, in_))
 
-    def pick(out, win, off):
-        op("v", [win, off], [out], lambda e: e.tensor_copy(ap(out), ap(win).indirect(ap(off))))
+    def flip(out, in_):
+        op("v", [in_], [out], lambda e: e.transpose(ap(out), ap(in_)), plain(out, in_))
+
+    def pick(out, win, off, q="v"):
+        cost = 0.06 + GATHER * size(out) * CYCLE
+        if q == "v":
+            op("v", [win, off], [out], lambda e: e.tensor_copy(ap(out), ap(win).indirect(ap(off))), cost)
+        else:
+            op("a", [win, off], [out], lambda e: e.activation(ap(out), ap(win).indirect(ap(off)), Fn.Copy), cost)
 
     def pick_less(out, win, off, in1):
-        op("v", [win, off, in1], [out], lambda e: e.tensor_tensor(ap(out), ap(win).indirect(ap(off)), ap(in1), Op.subtract))
+        op("v", [win, off, in1], [out], lambda e: e.tensor_tensor(ap(out), ap(win).indirect(ap(off)), ap(in1), Op.subtract),
+           0.05 + GATHER * size(out) * CYCLE)
 
-    def act(out, in_, f, bias=0.0, scale=1.0):
-        op("a", [in_], [out], lambda e: e.activation(ap(out), ap(in_), f, bias, scale))
+    def act(out, in_, f, bias=0.0, scale=1.0, more=0.0):
+        cols = [bias] if isinstance(bias, tuple) else []
+        b = ap(bias) if cols else bias
+        op("a", [in_] + cols, [out], lambda e: e.activation(ap(out), ap(in_), f, b, scale), 0.1 + more + size(out) * CYCLE)
 
     def mm(out, lhsT, rhs, start, stop, step=1):
         r = T[rhs[0]][:, rhs[1]:rhs[2]:step] if step > 1 else ap(rhs)
-        op("t", [lhsT, rhs], [out], lambda e: e.matmul(ap(out), ap(lhsT), r, start, stop))
+        op("t", [lhsT, rhs], [out], lambda e: e.matmul(ap(out), ap(lhsT), r, start, stop),
+           max(64, size(out)) * (4 if width(lhsT) == 4 else 1) * PE)
 
     def iota(out, pattern, base, cm, small=True):
+        cost = 0.13 + 2 * size(out) * CYCLE
         if small:
-            op("g", [], [out], lambda e: e.iota(ap(out), pattern, base, cm, allow_small_or_imprecise_dtypes=True))
+            op("g", [], [out], lambda e: e.iota(ap(out), pattern, base, cm, allow_small_or_imprecise_dtypes=True), cost)
         else:
-            op("g", [], [out], lambda e: e.iota(ap(out), pattern, base, cm))
+            op("g", [], [out], lambda e: e.iota(ap(out), pattern, base, cm), cost)
 
-    def send(to, out, in_, sem):
+    def copy_on(q, out, in_):
+        if q == "a":
+            act(out, in_, Fn.Copy)
+        elif q == "v":
+            cp(out, in_)
+        else:
+            op("g", [in_], [out], lambda e: e.affine_select(ap(out), ap(in_), [[0, size(out)]], Op.is_ge, 0.0, 0, 0),
+               0.17 + 2 * size(out) * CYCLE)
+
+    def send(to, out, in_, sem, left="sent", took=0.0, es=None, last=None):
         rid, pid = topo.addr(to, core)
-        es = [e for e in topo.engines(core, to) if e not in fold_es]
-        order("g", [in_], [])
-        g.remote_dma(ap(out), ap(in_), T.sem[sem], T.sem.sent, pid, rid, bits(es))
-        count["sent"] = count.get("sent", 0) + len(es)
+        es = es or [e for e in topo.engines(core, to) if e not in fold_es]
+        job("g", [in_], [("far", len(far), len(far) + 1)],
+            lambda e: e.remote_dma(ap(out), ap(in_), T.sem[sem], T.sem[left], pid, rid, bits(es)),
+            ISSUE, left, len(es), FAR + took + (0 if far else FIRST), True)
+        lands(last or sem, n_far, [out])
 
+    far = []
     helper = helper_of(core, T, topo)
     fold_es = fold_engines(core, T, topo)
     n_far = len(topo.engines(core, helper)) - len(fold_es)
@@ -197,74 +350,78 @@ def walk(g, core, rank, T, topo):
     def Ek(w, k):
         return (w, 128 - k, 256 - k)
 
-    RW, RGW, XW = ("R", 0, V), ("Rg", 0, V), ("Xs", K, K + V)
-    OC, GC, U, TL, Z1, W1, KEY, ZF, ZM, ZS, DUM, WC, T1, T2, CO, NUM = range(16)
-    IB, NIB, BIB, IF = ("Ib", 0, 128), ("nIb", 0, 128), ("bIb", 0, 128), ("If", 0, 128)
+    RW, XW, XZ = ("R", K, K + V), ("Xs", 16, 16 + V), ("X0", 0, V)
+    OC, J2, W1, KEY, DUM, WC, T1, CO, NUM, SC, CB = range(11)
+    IB, NIB, BIB, IF, BD = ("Ib", 0, 128), ("nIb", 0, 128), ("bIb", 0, 128), ("If", 0, 128), ("BD", 0, 128)
 
-    def turn(t, src, name):
-        a = 16 * t
-        dma("s", [(name, 0, V)], [RGW], T.Rg[0:128 - a, :], src[a:128, 0:V])
-        first = hist.pop("Rg")
-        dma("s", [(name, 0, V)], [RGW], T.Rg[128 - a:128, :], src[0:a, 0:V])
-        hist["Rg"] = first + hist["Rg"]
+    dma([], [("w0g", 0, 8)], T.w0g[16:128, 0:16], T.w0[0:112, :], 0.0)
+    dma([], [("w0g", 8, 16)], T.w0g[0:16, 0:16], T.w0[112:128, :], 0.0)
+    dma([], [("w0i", 0, 16)], T.w0i[:, :], T.w0[:, :], 0.0)
+    dma([], [RW], ap(RW), T.rec[:, :], 1.5)
 
-    dma("s", [], [("w0i", 0, 16)], T.w0i[:, :], T.w0[:, :])
-    dma("s", [], [RW], T.R[:, 0:V], T.rec[:, :])
-    dma("s", [], [("Xs", K - 1, K - 1 + V)], T.Xs[:, K - 1:K - 1 + V], T.x[:, :])
-    turn(1, T.rec, "rec")
+    dma([], [("Xs", 15, 15 + V)], T.Xs[:, 15:15 + V], T.x[:, :], 2.3)
+    dma([], [XZ], ap(XZ), T.x[:, :], 3.0)
 
-    iota(("Li", 0, 4), [[-1, 4]], 16, 1, False)
-    iota(("Li", 4, 5), [[0, 1]], 0, 1, False)
-    iota(("J", 0, 256), [[0, 2], [1, 128]], 0, 0)
+    iota(("J", 0, 128), [[1, 128]], 0, 0)
+    iota(("Li", 10, 11), [[0, 1]], 0, 17, False)
+    iota(("Li", 11, 12), [[0, 1]], 0, 2, False)
+    iota(("Li", 8, 9), [[0, 1]], 0, 16, False)
+    iota(("Li", 0, 8), [[-16, 2], [-1, 4]], 16, 1, False)
+    iota(Lf(J2), [[128, 2], [2, 8]], 0, 0)
     iota(("Gm", 0, 128), [[16, 8], [0, 16]], 0, 0)
+    send(T.cores[(rank + 1) % N], ("w0g", 16, 32), ("w0g", 0, 16), "ta0")
     iota(("Km", 0, 144), [[0, 9], [1, 16]], 0, 0)
-    iota(("thr", 0, K), [[1, K]], 0, 0)
-    iota(("R", V, 2048), [[0, 256]], 0, 0, False)
-    p_ = ("Li", 4, 5)
-    ts(("Li", 8, 12), ("Li", 0, 4), 15, None, Op.bitwise_and)
-    ts(("Li", 12, 13), p_, 112, None, Op.bitwise_and)
-    ts(("Li", 13, 14), p_, 7, None, Op.bitwise_and)
-    ts(("Li", 14, 15), p_, 3, 1, Op.arith_shift_right, Op.bitwise_and)
-    ts(("Li", 16, 17), p_, 4, 1, Op.arith_shift_right, Op.bitwise_and)
-    ts(("Li", 17, 18), p_, 1, None, Op.bitwise_and)
-    cp(("L", 16 * OC, 16 * OC + 7), ("Li", 8, 15))
-    cp(col(GC, 0), p_)
-    gcol, pcol, kcol, qcol, bcol, odd = col(OC, 4), col(GC, 0), col(OC, 0), col(OC, 5), col(OC, 6), col(GC, 1)
-    tt(odd, ("Li", 16, 17), ("Li", 17, 18), Op.not_equal)
-    ts(col(GC, 2), qcol, 16.0, bcol, Op.mult, Op.add)
-    ts(col(GC, 5), qcol, 0.0, odd, Op.is_equal, Op.mult)
-    ts(col(GC, 3), odd, 240.0, col(GC, 2), Op.mult, Op.add)
-    ts(col(GC, 4), col(GC, 5), 256.0, col(GC, 3), Op.mult, Op.add)
-    ts(("Lu", 8, 16), ("J", 64, 72), 2.0, col(GC, 3), Op.mult, Op.add)
-    ts(("Lu", 0, 8), ("J", 0, 8), 2.0, col(GC, 4), Op.mult, Op.add)
-    ts(IF, ("J", 0, 128), pcol, None, Op.is_equal)
-    ts(("Wb", 0, 256), ("J", 0, 256), gcol, None, Op.is_equal)
-    ts(("Wh", 0, 256), ("J", 0, 256), gcol, None, Op.is_equal)
-    ts(("BDb", 0, 128), ("Gm", 0, 128), gcol, None, Op.is_equal)
-    ts(("BDh", 0, 128), ("Gm", 0, 128), gcol, None, Op.is_equal)
-    ts(Lf(NUM), ("J", 0, 16), 16.0, kcol, Op.mult, Op.add)
-    for t in range(1, RO + 1):
-        ts(("Tq", 0, 128), ("Km", 16 - t, 144 - t), col(OC, t), -BIG, Op.is_gt, Op.mult)
-        tt(("Tri", 128 * (t - 1), 128 * t), ("Tq", 0, 128), ("BDb", 0, 128), Op.mult)
-    for n in sorted(set(NS_OWN[0] + NS_OWN[1] + NS_OWN[2])):
-        ts(col(CO, n), kcol, 4.0 * n, 4.0, Op.is_lt, Op.mult)
-    ts(col(CO, 8), kcol, 4.0 * NS_NEAR, 6.0, Op.is_lt, Op.mult)
-    ts(Lf(DUM), Lf(NUM), float(V + K - 1), None, Op.add)
-    act(IB, IF, Fn.Copy)
-    act(NIB, IF, Fn.Copy, 0.0, -1.0)
-    act(BIB, IF, Fn.Copy, 0.0, BIG)
-    act(("Wl", 0, 256), ("Wb", 0, 256), Fn.Copy, 0.0, 256.0)
-    act(Lf(WC), Lf(NUM), Fn.Exp, 128 * LNB, -LNB)
-    act(("thr", 0, K), ("thr", 0, K), Fn.Exp, 128 * LNB + math.log(2.55), -LNB)
+    iota(("R", 0, K), [[0, K]], 0, 0, False)
+    op("v", [], [("Rw", 0, 288)], lambda e: e.memset(T.Rw[:, :], 0.0), 0.27)
+    ts(("Li", 22, 24), ("Li", 10, 12), 4, 1, Op.arith_shift_right, Op.bitwise_and)
+    ts(("Li", 21, 22), ("Li", 8, 9), 112, None, Op.bitwise_and)
+    ts(("Li", 16, 20), ("Li", 0, 4), 15, None, Op.bitwise_and)
+    ts(("Li", 20, 21), ("Li", 4, 5), 112, None, Op.bitwise_and)
+    cp(("L", 16 * OC, 16 * OC + 8), ("Li", 16, 24))
+    kcol, gcol = col(OC, 0), col(OC, 4)
+    ts(col(OC, 8), col(OC, 6), 272.0, col(OC, 5), Op.mult, Op.add)
     cp(("q0", 256, 272), ("w0i", 0, 16))
-    cp(("q0", 272, 273), ("w0i", 0, 1))
-    ts(Lf(W1), ("w0i", 0, 16), float(K), 1.0 / BIG, Op.add, Op.mult)
+    ts(("Lu", 0, 16), Lf(J2), col(OC, 8), col(OC, 7), Op.add, Op.add)
+    ts(IF, ("J", 0, 128), kcol, gcol, Op.subtract, Op.is_equal)
+    ts(("Wb", 0, 128), ("J", 0, 128), gcol, None, Op.is_equal)
+    ts(Lf(NUM), ("J", 0, 16), 16.0, kcol, Op.mult, Op.add)
+    ts(BD, ("Gm", 0, 128), gcol, None, Op.is_equal)
+    ts(Lf(W1), ("w0i", 0, 16), K + 1 - 16 * LOW, None, Op.add)
+    ts(("L", 16 * SC, 16 * SC + 4), ("L", 16 * OC, 16 * OC + 4), -BIG, K - BIG, Op.mult, Op.add)
+    made = set()
 
-    late = []
+    def rows_col(i, n, val, add, k=None):
+        if not n:
+            return add
+        c = col(i, len([m for m in made if m[0] == i and m < (i, n, val, add)]))
+        for m in made:
+            if m[:4] == (i, n, val, add):
+                return m[4]
+        c = col(i, len([m for m in made if m[0] == i]))
+        made.add((i, n, val, add, c))
+        ts(c, kcol, 4.0 * n, val, Op.is_lt, Op.mult)
+        act(c, c, Fn.Identity, add)
+        return c
 
-    def run_late(n):
-        for _ in range(min(n, len(late))):
-            late.pop(0)()
+    act(("thf", 0, H), ("J", 0, H), Fn.Exp, 64 * LNB + math.log(2.55), -LNB, 1.3)
+    act(IB, IF, Fn.Copy)
+    act(("Ib", 128, 256), IF, Fn.Copy)
+
+    def more_constants():
+        act(("Wb", 128, 256), ("Wb", 0, 128), Fn.Copy)
+        act(("Wb", 256, 320), ("Wb", 0, 64), Fn.Copy)
+        act(NIB, IF, Fn.Copy, 0.0, -1.0)
+        act(BIB, IF, Fn.Copy, 0.0, BIG)
+        act(col(SC, RO), col(SC, RO), Fn.Identity, 1.0)
+        act(Lf(WC, 0), Lf(NUM, 0), Fn.Exp, 64 * LNB, -LNB)
+        act(("thr", 0, H), ("thf", 0, H), Fn.Copy)
+        act(("Wl", 0, 256), ("Wb", 0, 256), Fn.Copy, 0.0, -BIG / 16)
+        act(Lf(DUM), Lf(NUM), Fn.Identity, BIG)
+
+    def order_of_rows(t):
+        tq = ("Tq", 128 * (t - 1), 128 * t)
+        ts(tq, ("Km", 16 - t, 144 - t), col(OC, t), -BIG, Op.is_gt, Op.mult)
+        tt(("Tri", 128 * (t - 1), 128 * t), tq, BD, Op.mult)
 
     def ch(name, h, c, n=1):
         return (name, 2048 * h + 512 * c, 2048 * h + 512 * (c + n))
@@ -275,374 +432,332 @@ def walk(g, core, rank, T, topo):
     def hf(name, h, at=0):
         return (name, at + H * h, at + H * h + H)
 
-    def store(s):
-        dma("s", [("ss", K * s, K * s + K)], [], T.y[:, K * s:K * s + K], T.ss[:, K * s:K * s + K])
+    def reg(a, n=H):
+        return ("P", a, a + n)
+
+    def PB(c, n=1):
+        return reg(2048 + 512 * c, 512 * n)
+
+    CN = {F: reg(0), S: reg(1536)}
+    ZL = {F: reg(128, 8), S: reg(1664, 8)}
+    KR = {F: reg(256), S: reg(1792)}
+    CG = {F: reg(512), S: reg(640)}
+    CL = {F: reg(896), S: reg(768)}
+    VAL = {F: reg(1024), S: reg(0)}
+    NR = {F: reg(1152), S: reg(384)}
+    WL = reg(512, 16)
+
+    def ship(t):
+        send(relay_of(core, T, topo), ("Gh", V * (t - 2), V * (t - 1)), ("Rh", V * (t - 2), V * (t - 1)), "tin%d" % t, "sent",
+             2 * TABLE, fold_es, "tb%d" % t)
+
+    def narrowed(t, q):
+        for lo, hi in ((0, V // 2), (V // 2, V)):
+            copy_on(q, ("Rh", V * (t - 2) + lo, V * (t - 2) + hi), ("R", K + lo, K + hi))
+
+    def widened(t):
+        for lo, hi in ((0, V // 2), (V // 2, V)):
+            copy_on("g", ("G%d" % t, K + lo, K + hi), ("Gh", V * (t - 2) + lo, V * (t - 2) + hi))
 
     def step(t):
         s = t - 1
+        now[0] = t
         last = t == RO
         q, qn = "q%d" % s, "q%d" % t
         A = "A%d" % (s % 2)
         guest, asker = T.cores[(rank + t) % N], T.cores[(rank - t) % N]
         lq0 = 272 * s
-        ns = NS_OWN[s]
-        CN = [("P", 0, H), ("P", 512, 512 + H)]
-        ZL = [("P", 128, 136), ("P", 640, 648)]
-        KR = [("P", 256, 256 + H), ("P", 768, 768 + H)]
-        CG = [("P", 1024, 1024 + H), ("P", 1152, 1152 + H)]
-        VAL = [("P", 1536, 1536 + H), ("P", 1280, 1280 + H)]
-        NR = [("P", 1664, 1664 + H), ("P", 1792, 1792 + H)]
-        WL = ("P", 144, 160)
-        began = set()
+        asked, GW = ("lq", RW) if t == 1 else ("qs", ("G%d" % t, K, K + V))
+        new, goal = ("up", lq0, lq0 + K), ("up", lq0 + K, lq0 + 272)
 
-        def PB(c):
-            return ("P", 2048 + 512 * c, 2048 + 512 * c + 512)
+        def spread(e, name, h):
+            if h:
+                copy_on(e, (name, 640, 768), (name, 512, 640))
+                copy_on(e, (name, 768, 1024), (name, 512, 768))
+            else:
+                copy_on(e, (name, 256, 384), (name, 384, 512))
+                copy_on(e, (name, 0, 256), (name, 256, 512))
 
-        def spread(name, h, src=None):
-            a = 512 * h
-            if src is not None:
-                act((name, a, a + H), src, Fn.Copy)
-            act((name, a + H, a + 2 * H), src or (name, a, a + H), Fn.Copy)
-            act((name, a + 2 * H, a + 4 * H), (name, a, a + 2 * H), Fn.Copy)
+        def tally(out, d, h, chunks, back, close):
+            ks = [k for c in chunks for k in range(4 * c, 4 * c + 4)]
+            for i, k in enumerate(ks):
+                mm(out, Ek("Wb", k - back), row(d, h, k), i == 0, close and i == 15)
 
-        def own_pick(h, c):
-            o = 128 * h + 32 * c
-            pick_less(ch("dO", h, c), RW, (q, o, o + 32), ("R4", 512 * h, 512 * h + 512))
+        def likeness(d, h, names, o, wide, narrow, ns, out, back):
+            def test(c):
+                if c < ns:
+                    ts(ch(d, h, c), PB(bank[c]), C4, C4, Op.add, Op.is_equal)
+                else:
+                    ts(ch(d, h, c), ch(d, h, c), C4, C4, Op.add, Op.is_equal)
 
-        def guest_pick(h, c):
-            o = lq0 + 128 * h + 32 * c
-            pick_less(ch("dG", h, c), RGW, ("lq", o, o + 32), ("G4", 512 * h, 512 * h + 512))
+            bank, table = {}, GW if d == "dG" else RW
+            for c in range(ns):
+                bank[c] = turn[0] % 4
+                turn[0] += 1
+                got = ("gh", 512 * bank[c], 512 * bank[c] + 512)
+                pick(got, table, (names, o + 32 * c, o + 32 * c + 32), "a")
+                mm(PB(bank[c]), IB, got, True, False)
+                for i in range(4):
+                    mm(reg(PB(bank[c])[1] + H * i), NIB, hf(wide, h, 384), False, i == 3)
+            done = []
+            for c in range(ns, 4):
+                if c < ns + narrow:
+                    for k in range(4 * c, 4 * c + 4):
+                        pick_less(row(d, h, k), table, (names, o + 8 * k, o + 8 * k + 8), hf(wide, h, 384))
+                else:
+                    pick_less(ch(d, h, c), table, (names, o + 32 * c, o + 32 * c + 32), (wide, 512 * h, 512 * h + 512))
+                for e in ([c - 1] if c > ns else []) + ([c - ns] if c - ns < ns else []):
+                    test(e)
+                    done.append(e)
+            for c in [c for c in range(4) if c not in done]:
+                test(c)
+                done.append(c)
+            tally(out, d, h, done, back, d == "dG")
 
-        def test_v(d, h, c, n):
-            if n > 0:
-                ts(ch(d, h, c, n), ch(d, h, c, n), C4, C4, Op.add, Op.is_equal)
-
-        def test_s(h, c, n):
-            if n > 0:
-                act(ch("dO", h, c, n), ch("dO", h, c, n), Fn.Abs)
-                act(ch("dO", h, c, n), ch("dO", h, c, n), Fn.Sign, 2.5, -1.0)
-
-        def tally(out, d, h, c, n, total):
-            for k in range(4 * c, 4 * (c + n)):
-                m = len([1 for b in began if b[0] == out])
-                began.add((out, k))
-                mm(out, Ek("Wb", k), row(d, h, k), m == 0, m + 1 == total)
-
-        def guest_half(h):
-            for c in range(3):
-                guest_pick(h, c)
-            test_v("dG", h, 0, 2)
-            tally(CG[h], "dG", h, 0, 2, 16)
-            guest_pick(h, 3)
-            for c in (2, 3):
-                test_v("dG", h, c, 1)
-                tally(CG[h], "dG", h, c, 1, 16)
-
-        def answer(h):
-            act(hf("an", h, K * s), CG[h], Fn.Sign, -11.5)
-            send(asker, hf("la", h, K * s), hf("an", h, K * s), "aa%d" % (2 * s + h))
-
-        def x_pick(h, c, n=1):
-            out, o = ch("XC", h, c, n), 128 * h + 32 * c
-            off = (q, o, o + 32 * n)
-            op("a", [XW, off], [out], lambda e: e.activation(ap(out), ap(XW).indirect(ap(off)), Fn.Copy))
-
-        def x_load(h, c):
-            mm(PB(c), IB, ch("XC", h, c), True, False)
-
-        def x_less(h, c):
-            b = PB(c)[1]
-            for i in range(4):
-                mm(("P", b + H * i, b + H * i + H), NIB, hf("xz", h), False, i == 3)
-
-        def x_abs(h, c):
-            act(ch(A, h, c), PB(c), Fn.Abs)
-
-        def near_s(h, c, n=1):
-            act(ch("dO", h, c, n), ch(A, h, c, n), Fn.Sign, 0.5 + 2.0 ** -20, -1.0)
-
-        def near_v(h, c):
-            ts(ch("dO", h, c), PB(c), C1, C1, Op.add, Op.is_equal)
-
-        def twin(h):
-            mm(CN[h], BIB, hf("la", h, K * s), False, True)
-            ts(hf("twin", h), CN[h], col(CO, ns[h]), BIG + 11.5, Op.add, Op.is_ge)
-            mm(VAL[h], BIB, hf("twin", h), False, False)
-            mm(VAL[h], ("Tri", 128 * s, 128 * s + 128), hf("twin", h), False, True)
+        def serve(h):
+            ns = OPT["ns_guest"][s][h]
+            likeness("dG", h, asked, lq0 + H * h, "G4", OPT["gnarrow"] if h == F or t == 1 else 0, ns, CG[h], 16 * t)
+            if t == 1:
+                act(hf("an", h), CG[h], Fn.Sign, -11.5)
+                send(asker, hf("la", h), hf("an", h), "aa%d" % h)
+            else:
+                act(hf("la", h, K * s), CG[h], Fn.Sign, -11.5)
 
         def choose(h):
-            ts(hf("sel", h), VAL[h], K - BIG, 0.0, Op.add, Op.max)
+            ns = 0
+            mm(VAL[h], IB, hf("R4", h, 384) if last else hf("nn", h), True, False)
+            mm(CN[h], BIB, hf("la", h, K * s), False, True)
+            if OPT["twin"][h] == "a":
+                act(hf("twin", h), CN[h], Fn.Sign, rows_col(CO, ns, 4.0, -BIG - 11.5))
+                shift = col(SC, t)
+            else:
+                ts(hf("twin", h), CN[h], rows_col(CO, ns, -4.0, BIG + 11.5), 2.0, Op.is_ge, Op.mult)
+                shift = K + last - 2 * BIG
+            mm(VAL[h], BIB, hf("twin", h), False, False)
+            mm(VAL[h], ("Tri", 128 * s, 128 * s + 128), hf("twin", h), False, True)
+            ts(hf("sel", h), VAL[h], shift, -LOW, Op.add, Op.max)
             for r in range(16):
-                mm(ZL[h], Ek("Wh", r), ("sel", H * h + r, H * h + H), r == 0, r == 15, 16)
+                mm(ZL[h], Ek("Wb", r), ("sel", H * h + r, H * h + H), r == 0, r == 15, 16)
             if not last:
-                mm(KR[h], ("BDh", 0, 128), hf("sel", h), True, True)
+                mm(KR[h], BD, hf("sel", h), True, True)
+            j, jm, z = ("Li", 32 + 8 * h, 40 + 8 * h), ("Li", 48 + 8 * h, 56 + 8 * h), (qn, 256 + 8 * h, 264 + 8 * h)
+            tt(j, ZL[h], Lf(W1, h), Op.max)
+            ts(jm, j, 2047, None, Op.bitwise_and)
+            ts(z, jm, float(K), float(K), Op.max, Op.subtract)
+            pick(hf("xz", h), XZ, z, OPT["xz"][h])
+            if not last:
+                ts(Lf(KEY, h), ZL[h], 15 * LOW, None, Op.add)
+                ts(hf("key", h), KR[h], 15 * LOW, None, Op.add)
 
-        def after(h):
-            j16 = ("Lu", 16 + 8 * h, 24 + 8 * h)
-            tt(Lf(T2, h), ZL[h], Lf(NUM, h), Op.max)
-            cp(j16, Lf(T2, h))
-            pick(hf("xz", h), ("Xs", 0, K + V), j16)
+        def differ(h, c):
+            mm(PB(c), IB, ch("XC", h, c), True, False)
+            for i in range(4):
+                mm(reg(PB(c)[1] + H * i), NIB, hf("xz", h), False, i == 3)
 
-        def keys(h):
-            cp(Lf(KEY, h), ZL[h])
-            cp(hf("key", h), KR[h])
-            ts(Lf(U, h), Lf(KEY, h), 0.0, BIG, Op.is_equal, Op.mult)
+        def differs(h):
+            n = OPT["near"][h]
+            if h == F:
+                for c in (0, 2):
+                    differ(F, c)
+                    differ(F, c + 1)
+                    act(ch(A, F, c, 2), PB(c, 2), Fn.Abs)
+                return
+            for c in list(range(n)) + list(range(n, 4)):
+                differ(S, c)
+                if c >= n:
+                    ts(ch("nr", S, c), PB(c), C1, C1, Op.add, Op.is_equal)
+                if c == n - 1:
+                    act(ch(A, S, 0, n), PB(0, n), Fn.Abs)
 
-        at = [0]
+        def near(h):
+            n = OPT["near"][h]
+            if n:
+                act(ch("nr", h, 0, n), ch(A, h, 0, n), Fn.Sign, 0.5 + 2.0 ** -20, -1.0)
 
-        def claims(h, b0, b1):
-            for b in range(b0, b1):
-                lo = max(16 * b, H * h)
-                n = H * h + H - lo
-                e = ("dG", at[0], at[0] + n)
-                at[0] += n
-                ts(e, ("key", lo, lo + n), col(KEY, b), col(WC, b), Op.is_equal, Op.mult)
-                mm(("P", CN[h][2] - n, CN[h][2]), ("BDb", 0, 128), e, b == 0, b == 8 * h + 7)
+        def near_first():
+            n = OPT["near"][F]
+            for c in range(4 - n):
+                ts(ch("nr", F, c), ch(A, F, c), 0.5, None, Op.is_le)
+            for c, m in {0: [], 1: [(3, 1)], 2: [(2, 2)], 3: [(1, 1), (2, 2)], 4: [(0, 2), (2, 2)]}[n]:
+                act(ch("nr", F, c, m), ch(A, F, c, m), Fn.Sign, 0.5 + 2.0 ** -20, -1.0)
 
-        def loses(h):
-            tt(hf("win", h), CN[h], hf("thr", h), Op.is_ge)
+        def near_count(h):
+            n = OPT["near"][h]
+            if h == F:
+                return tally(NR[h], "nr", h, range(4), 0, True)
+            tally(NR[h], "nr", h, [n] + list(range(n)) + list(range(n + 1, 4)) if n < 4 and h == S else
+                  list(range(n, 4)) + list(range(n)), 0, True)
 
-        def listed():
-            mm(WL, IF, Lf(ZS), True, False)
-            for r in range(16):
-                mm(WL, Ek("Wl", r), ("win", r, K), False, r == 15, 16)
+        def claims(h):
+            mm(CL[h], NIB, ("thr", 0, H), True, False)
+            for b in range(8):
+                n = H - 16 * b
+                at = 576 * h + sum(H - 16 * i for i in range(b))
+                e = ("eq", at, at + n)
+                ts(e, ("key", H * h + 16 * b, H * h + H), col(KEY, 8 * h + b), col(WC, b), Op.is_equal, Op.mult)
+                mm(("P", CL[h][2] - n, CL[h][2]), BD, e, False, b == 7)
 
-        def place(i, h):
-            if i == 0:
-                tt(Lf(TL, h), Lf(U, h), Lf(W1, h), Op.mult)
-            if i == 1:
-                tt(Lf(Z1, h), Lf(KEY, h), Lf(TL, h), Op.add)
-            if i == 2:
-                ts(Lf(ZM, h), Lf(Z1, h), float(V + K - 1), -float(V), Op.is_ge, Op.mult)
-            if i == 3:
-                tt(Lf(ZF, h), Lf(ZM, h), Lf(Z1, h), Op.add)
-            if i == 4:
-                ts((qn, 256 + 8 * h, 264 + 8 * h), Lf(ZF, h), 1.0 - K, None, Op.add)
-                tt(Lf(ZS, h), Lf(ZF, h), Lf(U, h), Op.add)
-                ts(Lf(W1, h), Lf(ZF, h), 1.0, 1.0 / BIG, Op.add, Op.mult)
-                if h == 0:
-                    ts((qn, 272, 273), col(ZF, 0), 1.0 - K, None, Op.add)
-
-        def old(h):
+        def put(h):
             pick_less(hf("dl", h), RW, (qn, 256 + 8 * h, 264 + 8 * h), hf("nn", h))
+            n = OPT["near"][h]
+            bound = rows_col(CB, n, -6.0, 9.5) if h == S else rows_col(CB, 4 - n, 6.0, 3.5)
+            ts(NR[h], NR[h], bound, None, Op.is_lt)
+            tt(NR[h], NR[h], hf("dl", h), Op.mult)
+            tt(hf("up", h, lq0), NR[h], hf("nn", h), Op.add)
 
-        def target(i):
-            if i == 0:
-                tt(Lf(T1), WL, Lf(DUM), Op.min)
-            if i == 1:
-                ts(("Lu", 32, 48), Lf(T1), 1.0 - K, None, Op.add)
+        def write(table, name, at, to):
+            ts(("Lu", to, to + 16), (name, at + K, at + 272), -BIG, None, Op.add)
+            for h in (F, S):
+                off, src = ("Lu", to + 8 * h, to + 8 + 8 * h), hf(name, h, at)
+                op("v", [src, off], [(table, 0, 2048)],
+                   lambda e, off=off, src=src: e.tensor_copy(T[table][:, :].indirect(ap(off)), ap(src)),
+                   0.05 + SCATTER * H * CYCLE)
 
-        def write(h):
-            off = ("Lu", 32 + 8 * h, 40 + 8 * h)
-            op("v", [hf("nw", h), off], [("R", 0, 2048)], lambda e: e.tensor_copy(T.R[:, :].indirect(ap(off)), ap(hf("nw", h))))
-
-        def put(i, h):
-            if i == 0 and h == 0:
-                ts(NR[h], NR[h], 3.0, None, Op.is_lt)
-            if i == 0 and h == 1:
-                ts(NR[h], NR[h], col(CO, 8), 9.5, Op.add, Op.is_lt)
-            if i == 1:
-                tt(NR[h], NR[h], hf("dl", h), Op.mult)
-            if i == 2:
-                tt(hf("nw", h), NR[h], hf("nn", h), Op.add)
-
-        def expo(h, c, n):
+        def expo(h, c, n=1):
             act(ch(A, h, c, n), ch(A, h, c, n), Fn.Exp, 0.0, -1.0)
 
-        def fold():
+        def fold(h):
             rid, pid = topo.addr(helper, core)
-            order("g", [(A, 0, 4096)], [])
-            n = len(fold_es) // 2
-            trs = [RemoteDMATransfer(dst_ids=[DstId(rid=rid, pnc=pid)], dma_engine_mask=bits(fold_es[n * h:n * h + n]),
-                                     remote_sem=T.sem["hin%d" % s], srcs=[ap(row(A, h, k)) for k in range(16)],
-                                     dsts=[ap(hf("ss", h, K * s))], alu_op=1) for h in (0, 1)]
-            g.remote_dma_fused(trs, local_sem=T.sem["fold%d" % s])
-            count["fold%d" % s] = len(fold_es)
-            note("far", "fold%d" % s, len(fold_es), [(A, 0, 4096)], [])
-            lands("back%d" % s, len(topo.engines(helper, core)), [("ss", K * s, K * s + K)])
+            es = fold_es if h == F else [e for e in topo.engines(core, helper) if e not in fold_es]
+            trs = [RemoteDMATransfer(dst_ids=[DstId(rid=rid, pnc=pid)], dma_engine_mask=bits(es),
+                                     remote_sem=T.sem["hin%d" % (2 * s + h)], srcs=[ap(row(A, h, k)) for k in range(16)],
+                                     dsts=[ap(hf("ss", h, K * s))], alu_op=1)]
+            job("g", [ch(A, h, 0, 4)], [("far", len(far), len(far) + 1)],
+                lambda e: e.remote_dma_fused(trs, local_sem=T.sem["fold%d" % (2 * s + h)]), ISSUE, "fold%d" % (2 * s + h),
+                len(es), FOLD + FAR, True)
+            lands("back%d" % (2 * s + h), len(topo.engines(helper, core)), [hf("ss", h, K * s)])
+            if h == S:
+                ss = ("ss", K * s, K * s + K)
+                dma([ss], [], T.y[:, K * s:K * s + K], ap(ss), 0.3)
 
-        pick(("Rw", 0, 272), RW, (q, 256, 273))
-        op("v", [("Rw", 0, 256)], [("Tr", 0, 256)], lambda e: e.transpose(T.Tr[:, 0:256], T.Rw[:, 0:256]))
-        op("v", [("Rw", 16, 272)], [("Tr", 256, 512)], lambda e: e.transpose(T.Tr[:, 256:512], T.Rw[:, 16:272]))
-        spread("R4", 0, hf("Rw", 0))
-        pick((q, 0, 256), ("Tr", 0, 512), ("Lu", 0, 16))
-        send(guest, ("lq", lq0, lq0 + 272), (q, 0, 272), "qa%d" % s)
-        lands("qa%d" % s, n_far, [("lq", lq0, lq0 + 272)])
-        for h in (0, 1):
-            lands("aa%d" % (2 * s + h), n_far, [hf("la", h, K * s)])
-        if not last:
-            act(("rr", 0, K), ("Rw", 0, K), Fn.Relu, -float(V * (V - 2)), float(V))
-            mm(("P", 1024, 1280), IF, ("Rw", 0, K), True, False)
-            mm(("P", 1024, 1280), NIB, ("rr", 0, K), False, True)
-        mm(VAL[0], IF, hf("Rw", 0), True, False)
-        spread("R4", 1, hf("Rw", 1))
-        if not last:
-            act(("nn", 0, K), ("P", 1024, 1280), Fn.Identity, 1.0)
+        pick(("Rw", 16, 272), RW, (q, 256, 272))
+        flip(("Tr", 256, 544), ("Rw", 0, 288))
+        flip(("Tr", 0, 256), ("Rw", 16, 272))
+        pick(("qh", 0, 256), ("Tr", 0, 544), ("Lu", 0, 16))
+        mm(reg(1536, K), ("Ib", 128 - 16 * t, 256 - 16 * t), ("qh", 0, K), True, True)
+        cp(("qs", lq0, lq0 + K), reg(1536, K))
+        cp((q, 0, 256), ("qh", 0, 256))
+        copy_on(OPT["spread"][4], ("R4", 384, 640), ("Rw", 16, 272))
+        if OPT["ns_own"][s][F] + OPT["narrow"] < 4:
+            spread(OPT["spread"][0], "R4", F)
         if t == 1:
-            act(("Xs", K - 1 + V, K + V), ("Xs", K - 1, K), Fn.Copy)
-        run_late(99)
-        for c in range(4):
-            own_pick(0, c)
-        if EARLY:
-            own_pick(1, 0)
-        if t == 1:
-            test_s(0, 0, ns[0])
+            send(guest, ("lq", 0, K), ("qs", 0, K), "qa0")
+            ship(2)
+            act(("Xs", 15 + V, 16 + V), ("Xs", 15, 16), Fn.Copy)
+            cp(("lq", K, K + 16), ("w0g", 16, 32))
         else:
-            x_pick(0, 0)
-        for h in (0, 1):
-            pick(("G4", 512 * h, 512 * h + H), RGW, ("lq", lq0 + 256 + 8 * h, lq0 + 264 + 8 * h))
-            if h == 0:
-                spread("G4", 0)
-        test_v("dO", 0, ns[0], 4 - ns[0])
-        tally(CN[0], "dO", 0, ns[0], 4 - ns[0], 99)
-        spread("G4", 1)
+            write("G%d" % t, "lu", lq0 - 272, 32)
+        if t == 2:
+            narrowed(3, "g")
+            ship(3)
+        while early:
+            early.pop(0)()
+        pick(("G4", 384, 640), GW, (asked, lq0 + 256, lq0 + 272))
+        if OPT["ns_guest"][s][F] + OPT["gnarrow"] < 4:
+            spread(OPT["spread"][1], "G4", F)
+        while late:
+            late.pop(0)()
         if t == 1:
-            x_pick(0, 0, 2); x_pick(0, 2, 2)
+            spread(OPT["spread"][2], "R4", S)
+        if OPT["ns_guest"][s][S] + (OPT["gnarrow"] if t == 1 else 0) < 4:
+            spread(OPT["spread"][3], "G4", S)
+        if t > 1:
+            spread(OPT["spread"][2], "R4", S)
+        if not last:
+            iota(("G%d" % (t + 1), 0, K), [[0, K]], 0, 0)
+        if not last:
+            act(("rr", 0, K), ("Rw", 16, 272), Fn.Relu, -float(V * (V - 2)), float(V))
+            mm(reg(512, K), IB, ("R4", 384, 640), True, False)
+            mm(reg(512, K), NIB, ("rr", 0, K), False, True)
+            act(("nn", 0, K), reg(512, K), Fn.Identity, 1.0)
+        def states(h):
+            for c in range(4):
+                pick(ch("XC", h, c), XW, (q, H * h + 32 * c, H * h + 32 * c + 32), "a")
+
+        if t == 1:
+            serve(F)
+        likeness("dO", F, q, H * F, "R4", OPT["narrow"], OPT["ns_own"][s][F], CN[F], 0)
+        while late:
+            late.pop(0)()
+        serve(S if t == 1 else F)
+        if t == 1:
+            order_of_rows(1)
+        choose(F)
+        states(F)
+        if t > 1:
+            serve(S)
+        states(S)
+        likeness("dO", S, q, H * S, "R4", 0, OPT["ns_own"][s][S], CN[S], 0)
+        if t == 1:
+            for i in range(2, RO + 1):
+                order_of_rows(i)
+        if not last:
+            widened(t + 1)
+            differs(F)
+            choose(S)
+            differs(S)
+            near(S)
+            claims(F)
+            near_first()
+            ts(("qh", 256, 272), ("Li", 48, 64), float(K), float(K), Op.max, Op.subtract)
+            mm(reg(1920, 16), ("Ib", 112 - 16 * t, 240 - 16 * t), ("qh", 256, 272), True, True)
+            cp(("qs", lq0 + 528, lq0 + 544), reg(1920, 16))
+            claims(S)
+            act(("win", 0, K), reg(768, K), Fn.Sign)
+            near_count(F)
+            near_count(S)
+            mm(WL, IF, Lf(KEY), True, False)
+            for r in range(16):
+                mm(WL, Ek("Wl", r), ("win", r, K), False, r == 15, 16)
+            put(F)
+            tt(goal, WL, Lf(DUM), Op.max)
+            put(S)
+            ts(Lf(W1), ("Li", 48, 64), float(K), 1 - 16 * LOW, Op.max, Op.add)
+            send(T.cores[(rank - t - 1) % N], ("lu", lq0, lq0 + 272), ("up", lq0, lq0 + 272), "up%d" % t)
+            write("R", "up", lq0, 16)
+            n = OPT["near"][S]
+            behind("a", lambda: [act(ch(A, S, n, 4 - n), PB(n, 4 - n), Fn.Abs)] + [expo(F, c, 2) for c in (0, 2)])
+            early.append(lambda: fold(F))
+            late.extend([lambda c=c: expo(S, c, 2) for c in (0, 2)] + [lambda: fold(S)])
         else:
-            test_s(0, 0, ns[0])
-            x_pick(0, 1)
-        guest_half(0)
-        answer(0)
-        tally(CN[0], "dO", 0, 0, ns[0], 99)
-        if t > 1:
-            x_pick(0, 2, 2)
-        op("a", [XW, (q, 256, 272)], [("Xs", 0, K)],
-           lambda e: e.activation(T.Xs[:, 0:K], ap(XW).indirect(ap((q, 256, 272))), Fn.Copy))
-        x_pick(1, 0, 2)
-        if t == 1:
-            x_pick(1, 2)
-        for c in range(4):
-            x_load(0, c)
-        guest_half(1)
-        answer(1)
-        if last:
-            store(s - 1)
-        twin(0)
-        mm(VAL[1], IF, hf("Rw", 1), True, False)
-        early = EARLY
-        own_pick(1, early)
-        if t > 1:
-            x_pick(1, 2)
-        test_s(1, 0, ns[1])
-        x_pick(1, 3)
-        choose(0)
-        own_pick(1, early + 1)
-        after(0)
-        for c in range(4):
-            x_less(0, c)
-            x_abs(0, c)
-            if c == 1 and not last:
-                near_s(0, 0, 2)
-        if not last:
-            keys(0)
-        if not early:
-            own_pick(1, 2)
-        tally(CN[1], "dO", 1, 0, ns[1], 99)
-        test_v("dO", 1, ns[1], 2 + early - ns[1])
-        tally(CN[1], "dO", 1, ns[1], 2 + early - ns[1], 99)
-        if not early:
-            x_load(1, 0); x_load(1, 1)
-        own_pick(1, 3)
-        for c in range(2 + early, 4):
-            test_v("dO", 1, c, 1)
-            tally(CN[1], "dO", 1, c, 1, 99)
-        if not last:
-            near_s(0, 2, 2)
-            place(0, 0)
-            claims(0, 0, 2)
-            place(1, 0)
-            claims(0, 2, 4)
-            place(2, 0)
-            twin(1)
-            if early:
-                x_load(1, 0); x_load(1, 1)
-            else:
-                tally(NR[0], "dO", 0, 0, 2, 16)
-            place(3, 0)
-            claims(0, 4, 8)
-            place(4, 0)
-            choose(1)
-            if early:
-                tally(NR[0], "dO", 0, 0, 2, 16)
-            x_load(1, 2); x_load(1, 3)
-            old(0)
-            loses(0)
-            after(1)
+            SUM = NR[F]
+            for c in (0, 2):
+                differ(F, c)
+                differ(F, c + 1)
+                act(ch(A, F, c, 2), PB(c, 2), Fn.Abs)
+            choose(S)
+            expo(F, 0, 2)
+            act(PB(2, 2), ch(A, F, 2, 2), Fn.Exp, 0.0, -1.0)
+            a, b = ch(A, F, 2)[1], PB(2)[1]
+            tt((A, a, a + 512), PB(3), ch(A, F, 1), Op.add)
+            tt(PB(2), PB(2), ch(A, F, 0), Op.add)
+            tt((A, a + 512, a + 768), reg(b + K, K), (A, a + K, a + 512), Op.add)
+            tt(reg(1152, K), reg(b, K), (A, a, a + K), Op.add)
             for c in (0, 1, 3, 2):
-                x_less(1, c)
-            keys(1)
-            x_abs(1, 0)
-            for c in range(NS_NEAR):
-                if c + 1 < NS_NEAR:
-                    x_abs(1, c + 1)
-                near_s(1, c)
-            tally(NR[0], "dO", 0, 2, 2, 16)
-            for i in range(4):
-                claims(1, 2 * i, 2 * i + 2)
-                place(i, 1)
-            claims(1, 8, 16)
-            place(4, 1)
-            put(0, 0)
-            for c in range(NS_NEAR, 4):
-                near_v(1, c)
-            put(1, 0)
-            loses(1)
-            listed()
-            put(2, 0)
-            old(1)
-            tally(NR[1], "dO", 1, 0, min(2, NS_NEAR), 16)
-            tally(NR[1], "dO", 1, NS_NEAR, 4 - NS_NEAR, 16)
-            tally(NR[1], "dO", 1, 2, NS_NEAR - 2, 16)
-            target(0); target(1)
-            write(0)
-            put(0, 1); put(1, 1); put(2, 1)
-            write(1)
-            turn(t + 1, T.R, "R")
-            if s > 0:
-                store(s - 1)
-            for c in range(NS_NEAR, 4):
-                x_abs(1, c)
-            expo(0, 0, 2); expo(0, 2, 2)
-            late.extend([lambda: expo(1, 0, 2), lambda: expo(1, 2, 2), fold])
-        else:
-            expo(0, 0, 2); expo(0, 2, 2)
-            twin(1)
-            if early:
-                x_load(1, 0); x_load(1, 1)
-            choose(1)
-            x_load(1, 2); x_load(1, 3)
-            for k in range(2):
-                mm(CN[0], IF, row(A, 0, k), k == 0, k == 15)
-            after(1)
-            for c in (0, 3, 1, 2):
-                x_less(1, c)
-            for k in range(2, 16):
-                mm(CN[0], IF, row(A, 0, k), k == 0, k == 15)
-            ts(("acc", 512, 1024), PB(3), -1.0, None, Op.mult)
-            tt(ch(A, 1, 3), PB(3), ("acc", 512, 1024), Op.max)
-            for i, c in enumerate((0, 3, 1, 2)):
-                if c != 3:
-                    x_abs(1, c)
-                a, b = ch(A, 1, c)[1], PB(c)[1]
-                if i == 0:
-                    act(("acc", 0, K), (A, a, a + K), Fn.Exp, 0.0, -1.0)
-                    act(("P", b, b + K), (A, a + K, a + 2 * K), Fn.Exp, 0.0, -1.0)
-                    tt(("acc", 0, K), ("P", b, b + K), ("acc", 0, K), Op.add)
-                elif i < 3:
-                    act(PB(c), ch(A, 1, c), Fn.Exp, 0.0, -1.0)
-                    tt(("acc", 0, K), ("P", b, b + K), ("acc", 0, K), Op.add)
-                    tt(("acc", 0, K), ("P", b + K, b + 2 * K), ("acc", 0, K), Op.add)
-                else:
-                    b2 = PB(0)[1]
-                    act(("P", b, b + K), (A, a, a + K), Fn.Exp, 0.0, -1.0)
-                    act(("P", b2, b2 + K), (A, a + K, a + 2 * K), Fn.Exp, 0.0, -1.0)
-                    tt(("acc", 0, K), ("P", b, b + K), ("acc", 0, K), Op.add)
-                    cp(hf("yo", 0), CN[0])
-                    tt(("acc", 0, K), ("P", b2, b2 + K), ("acc", 0, K), Op.add)
-            tt(hf("yo", 1), ("acc", 0, H), ("acc", H, K), Op.add)
-            dma("s", [("yo", 0, K)], [], T.y[:, K * s:K * s + K], T.yo[:, :])
+                differ(S, c)
+            act(ch(A, S, 0, 2), PB(0, 2), Fn.Abs)
+            for c in (3, 2):
+                ts(("acc", 0, 512), PB(c), -1.0, None, Op.mult)
+                tt(ch(A, S, c), PB(c), ("acc", 0, 512), Op.max)
+            tt((A, a, a + H), reg(1152), (A, a + 512, a + 640), Op.add)
+            tt(reg(1152), reg(1280), (A, a + 640, a + 768), Op.add)
+            tt(hf("yo", F), reg(1152), (A, a, a + H), Op.add)
+            expo(S, 0, 2)
+            for k in range(8):
+                mm(NR[S], IF, row(A, S, k), k == 0, k == 7)
+            expo(S, 2)
+            act(PB(3), ch(A, S, 3), Fn.Exp, 0.0, -1.0)
+            a, b = ch(A, S, 2)[1], PB(3)[1]
+            tt(("acc", 0, K), reg(b, K), (A, a, a + K), Op.add)
+            tt(reg(b + K, K), reg(b + K, K), (A, a + K, a + 2 * K), Op.add)
+            tt(("acc", K, K + H), reg(b + K), ("acc", 0, H), Op.add)
+            tt(reg(b), reg(b + K + H), ("acc", H, K), Op.add)
+            tt(("acc", K, K + H), reg(b), ("acc", K, K + H), Op.add)
+            tt(hf("yo", S), NR[S], ("acc", K, K + H), Op.add)
+            dma([("yo", 0, K)], [], T.y[:, K * s:K * s + K], T.yo[:, :], 0.3)
 
+    narrowed(2, "a")
+    more_constants()
     for t in range(1, RO + 1):
         step(t)
-    for sem, n in count.items():
-        need("s", sem, n, {})
+    return jobs

import math
from concourse.bass import DstId, RemoteDMATransfer
from concourse.mybir import AluOpType as Op, ActivationFunctionType as Fn

V, K, RO, H = 1792, 256, 3, 128
F, S = 1, 0
BIG = 4096.0
LOW = 2048.0
C4 = 1.5 * 2.0 ** 25
C1 = 1.5 * 2.0 ** 23
LNB = 0.5 * math.log(3.0)
OPT = {"ns_own": ((0, 0), (0, 2), (0, 2)), "ns_guest": ((3, 3), (1, 3), (1, 3)), "near": (1, 4), "narrow": 0,
       "spread": "vvgvg", "shift": {}, "twin": "va", "xz": "va", "slack": 0.07, "rounds": 0, "gnarrow": 0, "hold": 9.0, "gap": 0.5}
CYCLE, PE, GATHER, SCATTER, WAKE, NEAR, FAR, FIRST, FOLD = 0.00083, 0.0005, 1.6, 3.0, 0.09, 1.3, 1.9, 2.0, 12.0
TABLE, ISSUE = 6.0, 1.0
PLAN = {}

SCRATCH = {
    "Rh": ("sbuf", [128, 2 * V], "float16"), "Gh": ("sbuf", [128, 2 * V], "float16"),
    "G2": ("sbuf", [128, 2048], "float32"), "G3": ("sbuf", [128, 2048], "float32"), "up": ("sbuf", [128, 544], "float32"),
    "lu": ("sbuf", [128, 544], "float32"), "R": ("sbuf", [128, 2048], "int32"), "qh": ("sbuf", [128, 272], "float16"), "qs": ("sbuf", [128, 3 * 272], "uint16"),
    "Xs": ("sbuf", [128, V + 16], "bfloat16"), "X0": ("sbuf", [128, V], "bfloat16"), "w0i": ("sbuf", [128, 16], "int32"),
    "q0": ("sbuf", [128, 272], "uint16"), "q1": ("sbuf", [128, 272], "uint16"), "q2": ("sbuf", [128, 272], "uint16"),
    "q3": ("sbuf", [128, 272], "uint16"), "w0g": ("sbuf", [128, 32], "int32"),
    "lq": ("sbuf", [128, 3 * 272], "uint16"), "an": ("sbuf", [128, 768], "bfloat16"), "la": ("sbuf", [128, 768], "bfloat16"),
    "Rw": ("sbuf", [128, 288], "float32"), "R4": ("sbuf", [128, 1024], "float16"), "G4": ("sbuf", [128, 1024], "float16"),
    "Tr": ("sbuf", [128, 544], "float32"),
    "dO": ("sbuf", [128, 4096], "bfloat16"), "dG": ("sbuf", [128, 4096], "bfloat16"), "XC": ("sbuf", [128, 4096], "bfloat16"),
    "gh": ("sbuf", [128, 2048], "float16"), "nr": ("sbuf", [128, 4096], "bfloat16"), "eq": ("sbuf", [128, 1152], "bfloat16"),
    "A0": ("sbuf", [128, 4096], "float32"), "A1": ("sbuf", [128, 4096], "float32"),
    "twin": ("sbuf", [128, K], "bfloat16"), "sel": ("sbuf", [128, K], "float16"), "key": ("sbuf", [128, K], "float16"),
    "xz": ("sbuf", [128, K], "bfloat16"), "rr": ("sbuf", [128, K], "bfloat16"), "nn": ("sbuf", [128, K], "float16"),
    "dl": ("sbuf", [128, K], "float32"),
    "win": ("sbuf", [128, K], "bfloat16"), "thf": ("sbuf", [128, H], "float32"), "thr": ("sbuf", [128, H], "bfloat16"),
    "L": ("sbuf", [128, 192], "float32"), "Li": ("sbuf", [128, 64], "int32"), "Lu": ("sbuf", [128, 48], "uint16"),
    "ss": ("sbuf", [128, 512], "float32"), "acc": ("sbuf", [128, 1024], "float32"), "yo": ("sbuf", [128, K], "float32"),
    "J": ("sbuf", [128, 128], "float32"), "Km": ("sbuf", [128, 144], "bfloat16"), "Gm": ("sbuf", [128, 128], "bfloat16"),
    "Wb": ("sbuf", [128, 320], "bfloat16"), "Wl": ("sbuf", [128, 256], "bfloat16"), "BD": ("sbuf", [128, 128], "bfloat16"),
    "Ib": ("sbuf", [128, 256], "bfloat16"), "nIb": ("sbuf", [128, 128], "bfloat16"), "bIb": ("sbuf", [128, 128], "bfloat16"),
    "If": ("sbuf", [128, 128], "float32"), "Tri": ("sbuf", [128, 384], "bfloat16"), "Tq": ("sbuf", [128, 384], "bfloat16"),
    "P": ("psum", [128, 4096], "float32"),
}
NDMA = 16
SEMAPHORES = (["sv", "sa", "st", "sg", "sent", "ta0", "qa0", "aa0", "aa1", "up1", "up2"]
              + ["%s%d" % (n, t) for n in ("tin", "tb") for t in (2, 3)]
              + [n + str(i) for n in ("fold", "hin", "back") for i in range(4)] + ["d%d" % i for i in range(NDMA)])


def helper_of(core, T, topo):
    for c in topo.cores_of(core):
        if c != core and T.rank_of(c) is None and topo.die(c) == topo.die(core):
            return c
    return None


def asker_of(core, t, T):
    return T.cores[(T.rank_of(core) - t) % len(T.cores)]


def relay_of(core, T, topo):
    for c in topo.cores_of(core):
        if (T.rank_of(c) is None and topo.die(c) == topo.die(core) and c != helper_of(core, T, topo)
                and all(topo.may_write(c, asker_of(core, t, T)) for t in (2, 3))):
            return c
    return None


def hand_on(g, core, owner, T, topo):
    near = fold_engines(owner, T, topo)
    for t in (2, 3):
        to = asker_of(owner, t, T)
        rid, pid = topo.addr(to, core)
        es = [e for e in topo.engines(core, to) if e not in near]
        g.wait_ge(T.sem["tin%d" % t], len(near))
        lists = T.Gh[:, V * (t - 2):V * (t - 1)]
        g.remote_dma(lists, lists, T.sem["tb%d" % t], T.sem.sent, pid, rid, bits(es))
    g.wait_ge(T.sem.sent, 2 * len(es))


def bits(engines):
    m = 0
    for e in engines:
        m |= 1 << e
    return m


def rank_program(g, core, T, topo):
    rank = T.rank_of(core)
    if rank is None:
        for c in T.cores:
            if helper_of(c, T, topo) == core:
                hand_back(g, core, c, T, topo)
            if relay_of(c, T, topo) == core:
                hand_on(g, core, c, T, topo)
        return
    jobs = walk(g, core, rank, T, topo)
    if "order" not in PLAN:
        PLAN["order"] = arrange(jobs)
    issue(g, T, [jobs[i] for i in PLAN["order"]])


def fold_engines(core, T, topo):
    far = [c for c in T.cores if c not in topo.cores_of(core)][0]
    return [e for e in topo.engines(core, helper_of(core, T, topo)) if e not in topo.engines(core, far)]


def hand_back(g, core, owner, T, topo):
    rid, pid = topo.addr(owner, core)
    n = len(fold_engines(owner, T, topo))
    m = topo.mask(core, owner)
    for i in [2 * s + h for s in range(RO - 1) for h in (F, S)]:
        g.wait_ge(T.sem["hin%d" % i], n)
        half = T.ss[:, i * H:i * H + H]
        g.remote_dma(half, half, T.sem["back%d" % i], T.sem.sent, pid, rid, m)
    g.wait_ge(T.sem.sent, 2 * (RO - 1) * len(topo.engines(core, owner)))


def earlier(hist, q, reads, writes, plan):
    found = []
    for rs, w in ((reads, False), (writes, True)):
        for name, lo, hi in rs:
            for lo2, hi2, w2, q2, mark in hist.get(name, []):
                if name == "P" and (q2 != q or q == "t"):
                    hit = (plan or q2 != q) and lo // 512 <= (hi2 - 1) // 512 and lo2 // 512 <= (hi - 1) // 512
                else:
                    hit = lo < hi2 and lo2 < hi and (w or w2)
                if hit:
                    found.append(mark)
    return found


def remember(hist, q, reads, writes, mark):
    for rs, w in ((reads, False), (writes, True)):
        for name, lo, hi in rs:
            h = hist.setdefault(name, [])
            if w:
                h[:] = [e for e in h if not (lo <= e[0] and e[1] <= hi and (name != "P" or e[3] == q))]
            h.append((lo, hi, w, q, mark))


def arrange(jobs):
    hist, deps = {}, []
    for i, j in enumerate(jobs):
        deps.append(set(earlier(hist, j["q"], j["reads"], j["writes"], True)))
        remember(hist, j["q"], j["reads"], j["writes"], i)
    behind = {(p, i) for i, j in enumerate(jobs) for p in j["behind"] if p not in deps[i]}
    for p, i in behind:
        deps[i].add(p)
    users = [[] for _ in jobs]
    for i, d in enumerate(deps):
        for p in d:
            users[p].append(i)

    def gap(p, i):
        if (p, i) in behind:
            return 0.0
        return jobs[p]["late"] + (0.0 if jobs[p]["q"] == jobs[i]["q"] == "t" else WAKE)

    def run(before, after, urgency, wait, forward, timed=True):
        left = [len(d) for d in before]
        ready = {i: 0.0 if forward else jobs[i]["late"] for i in range(len(jobs)) if not before[i]}
        free, done, order = {}, [0.0] * len(jobs), []
        due, lag = {}, 0.0
        if timed:
            for i in sorted(range(len(jobs)), key=lambda i: urgency[i]):
                due.setdefault(jobs[i]["q"], []).append(i)
            top = max(urgency)

        def in_the_way(c, at):
            u = due[jobs[c]["q"]][-1]
            return u != c and top - urgency[u] + lag < at + jobs[c]["cost"] - OPT["hold"] and urgency[u] > urgency[c] + OPT["gap"]

        while ready:
            start = {i: max(r, free.get(jobs[i]["q"], 0.0)) for i, r in ready.items()}
            able = [i for i in ready if not timed or not in_the_way(i, start[i])] or list(ready)
            first = min(able, key=lambda i: (start[i], -urgency[i], i))
            q = jobs[first]["q"]
            i = max([c for c in able if jobs[c]["q"] == q and start[c] <= start[first] + OPT["slack"]],
                    key=lambda c: (urgency[c], -c))
            done[i] = free[q] = start[i] + jobs[i]["cost"]
            if timed:
                due[q].remove(i)
                lag = max(lag, start[i] - top + urgency[i])
            order.append(i)
            del ready[i]
            for u in after[i]:
                left[u] -= 1
                if left[u] == 0:
                    ready[u] = max([done[p] + wait(p, u) for p in before[u]] + [0.0 if forward else jobs[u]["late"]])
        return max(d + (j["late"] if forward else 0.0) for d, j in zip(done, jobs)), order, done

    best = run(deps, users, [OPT["shift"].get(j["tag"], 0) - i for i, j in enumerate(jobs)], gap, True, False)
    last = best
    for _ in range(OPT["rounds"]):
        back = run(users, deps, last[2], lambda p, u: gap(u, p), False)
        last = run(deps, users, back[2], gap, True)
        best = min(best, last)
    return best[1]


def issue(g, T, jobs):
    eng = {"v": g.vector, "a": g.scalar, "t": g.tensor, "g": g, "s": g.sync}
    count = {}
    known = {q: {} for q in eng}
    hist = {}

    def need(q, sem, val, kn):
        if known[q].get(sem, 0) >= val:
            return
        eng[q].wait_ge(T.sem[sem], val)
        known[q][sem] = val
        for s, n in kn.items():
            if known[q].get(s, 0) < n:
                known[q][s] = n

    for j in jobs:
        q, sem = j["q"], j["sem"]
        if q in eng:
            for val, s, kn in sorted(earlier(hist, q, j["reads"], j["writes"], False), key=lambda d: -d[0]):
                need(q, s, val, kn)
            made = j["call"](eng[q])
            if not j["remote"]:
                made.then_inc(T.sem[sem], j["inc"])
        count[sem] = count.get(sem, 0) + j["inc"]
        mine = [r for r in j["writes"] if r[0] != "far"]
        if sem != "sent":
            remember(hist, q, [r for r in j["reads"] if r[0] != "far"], mine, (count[sem], sem, dict(known.get(q, {}))))
    for sem, n in count.items():
        need("s", sem, n, {})


def walk(g, core, rank, T, topo):
    N = len(T.cores)
    jobs = []
    ndma = [0]
    held, now = {}, [0]
    late, early, turn = [], [], [0]

    def job(q, reads, writes, call, cost, sem, inc, late=0.0, remote=False):
        jobs.append({"q": q, "reads": reads, "writes": writes, "call": call, "cost": cost, "sem": sem, "inc": inc,
                     "late": late, "remote": remote, "behind": held.get(q, [])[-1:],
                     "tag": (now[0], q, writes[0][0], reads[0][0] if q != "t" else reads[1][0],
                             (writes[0] if q != "t" else reads[1])[1] * 2 // SCRATCH[(writes[0] if q != "t" else reads[1])[0]][1][1])
                     if q in "vat" and reads else None})
        if q == "g":
            held[q] = [len(jobs) - 1]

    def behind(q, calls):
        held[q] = [max(i for i, j in enumerate(jobs) if j["q"] == q)]
        calls()
        del held[q]

    def op(q, reads, writes, call, cost):
        job(q, reads, writes, call, cost, "s" + q, 1)

    def width(r):
        return 4 if SCRATCH[r[0]][2] in ("float32", "int32") else 2

    def size(r):
        return r[2] - r[1]

    def dma(reads, writes, out, in_, took):
        job("s", reads, writes, lambda e: e.dma_start(out, in_), 0.05, "d%d" % ndma[0], 16, NEAR + took)
        ndma[0] += 1

    def lands(sem, n, writes):
        job("far" + sem, [("far", len(far), len(far) + 1)], writes, None, 0.001, sem, n)
        far.append(sem)

    def ap(r):
        return T[r[0]][:, r[1]:r[2]]

    def plain(out, in_):
        return 0.03 + max(64, size(out) * (0.5 if width(out) == width(in_) == 2 else 1)) * CYCLE

    def ts(out, in0, s1, s2, o0, o1=None):
        cols = [s for s in (s1, s2) if isinstance(s, tuple)]
        a1, a2 = [ap(s) if isinstance(s, tuple) else s for s in (s1, s2)]
        if o1 is None:
            op("v", [in0] + cols, [out], lambda e: e.tensor_scalar(ap(out), ap(in0), a1, None, o0), plain(out, in0))
        else:
            op("v", [in0] + cols, [out], lambda e: e.tensor_scalar(ap(out), ap(in0), a1, a2, o0, o1), plain(out, in0))

    def tt(out, in0, in1, o):
        op("v", [in0, in1], [out], lambda e: e.tensor_tensor(ap(out), ap(in0), ap(in1), o),
           0.03 + max(64, size(out) * (1 if "P" in (in0[0], in1[0]) else 2)) * CYCLE)

    def cp(out, in_):
        op("v", [in_], [out], lambda e: e.tensor_copy(ap(out), ap(in_)), plain(out, in_))

    def flip(out, in_):
        op("v", [in_], [out], lambda e: e.transpose(ap(out), ap(in_)), plain(out, in_))

    def pick(out, win, off, q="v"):
        cost = 0.06 + GATHER * size(out) * CYCLE
        if q == "v":
            op("v", [win, off], [out], lambda e: e.tensor_copy(ap(out), ap(win).indirect(ap(off))), cost)
        else:
            op("a", [win, off], [out], lambda e: e.activation(ap(out), ap(win).indirect(ap(off)), Fn.Copy), cost)

    def pick_less(out, win, off, in1):
        op("v", [win, off, in1], [out], lambda e: e.tensor_tensor(ap(out), ap(win).indirect(ap(off)), ap(in1), Op.subtract),
           0.05 + GATHER * size(out) * CYCLE)

    def act(out, in_, f, bias=0.0, scale=1.0, more=0.0):
        cols = [bias] if isinstance(bias, tuple) else []
        b = ap(bias) if cols else bias
        op("a", [in_] + cols, [out], lambda e: e.activation(ap(out), ap(in_), f, b, scale), 0.1 + more + size(out) * CYCLE)

    def mm(out, lhsT, rhs, start, stop, step=1):
        r = T[rhs[0]][:, rhs[1]:rhs[2]:step] if step > 1 else ap(rhs)
        op("t", [lhsT, rhs], [out], lambda e: e.matmul(ap(out), ap(lhsT), r, start, stop),
           max(64, size(out)) * (4 if width(lhsT) == 4 else 1) * PE)

    def iota(out, pattern, base, cm, small=True):
        cost = 0.13 + 2 * size(out) * CYCLE
        if small:
            op("g", [], [out], lambda e: e.iota(ap(out), pattern, base, cm, allow_small_or_imprecise_dtypes=True), cost)
        else:
            op("g", [], [out], lambda e: e.iota(ap(out), pattern, base, cm), cost)

    def copy_on(q, out, in_):
        if q == "a":
            act(out, in_, Fn.Copy)
        elif q == "v":
            cp(out, in_)
        else:
            op("g", [in_], [out], lambda e: e.affine_select(ap(out), ap(in_), [[0, size(out)]], Op.is_ge, 0.0, 0, 0),
               0.17 + 2 * size(out) * CYCLE)

    def send(to, out, in_, sem, left="sent", took=0.0, es=None, last=None):
        rid, pid = topo.addr(to, core)
        es = es or [e for e in topo.engines(core, to) if e not in fold_es]
        job("g", [in_], [("far", len(far), len(far) + 1)],
            lambda e: e.remote_dma(ap(out), ap(in_), T.sem[sem], T.sem[left], pid, rid, bits(es)),
            ISSUE, left, len(es), FAR + took + (0 if far else FIRST), True)
        lands(last or sem, n_far, [out])

    far = []
    helper = helper_of(core, T, topo)
    fold_es = fold_engines(core, T, topo)
    n_far = len(topo.engines(core, helper)) - len(fold_es)

    def Lf(i, h=None):
        return ("L", 16 * i, 16 * i + 16) if h is None else ("L", 16 * i + 8 * h, 16 * i + 8 * h + 8)

    def col(i, j):
        return ("L", 16 * i + j, 16 * i + j + 1)

    def Ek(w, k):
        return (w, 128 - k, 256 - k)

    RW, XW, XZ = ("R", K, K + V), ("Xs", 16, 16 + V), ("X0", 0, V)
    OC, J2, W1, KEY, DUM, WC, T1, CO, NUM, SC, CB = range(11)
    IB, NIB, BIB, IF, BD = ("Ib", 0, 128), ("nIb", 0, 128), ("bIb", 0, 128), ("If", 0, 128), ("BD", 0, 128)

    dma([], [("w0g", 0, 8)], T.w0g[16:128, 0:16], T.w0[0:112, :], 0.0)
    dma([], [("w0g", 8, 16)], T.w0g[0:16, 0:16], T.w0[112:128, :], 0.0)
    dma([], [("w0i", 0, 16)], T.w0i[:, :], T.w0[:, :], 0.0)
    dma([], [RW], ap(RW), T.rec[:, :], 1.5)

    dma([], [("Xs", 15, 15 + V)], T.Xs[:, 15:15 + V], T.x[:, :], 2.3)
    dma([], [XZ], ap(XZ), T.x[:, :], 3.0)

    iota(("J", 0, 128), [[1, 128]], 0, 0)
    iota(("Li", 10, 11), [[0, 1]], 0, 17, False)
    iota(("Li", 11, 12), [[0, 1]], 0, 2, False)
    iota(("Li", 8, 9), [[0, 1]], 0, 16, False)
    iota(("Li", 0, 8), [[-16, 2], [-1, 4]], 16, 1, False)
    iota(Lf(J2), [[128, 2], [2, 8]], 0, 0)
    iota(("Gm", 0, 128), [[16, 8], [0, 16]], 0, 0)
    send(T.cores[(rank + 1) % N], ("w0g", 16, 32), ("w0g", 0, 16), "ta0")
    iota(("Km", 0, 144), [[0, 9], [1, 16]], 0, 0)
    iota(("R", 0, K), [[0, K]], 0, 0, False)
    op("v", [], [("Rw", 0, 288)], lambda e: e.memset(T.Rw[:, :], 0.0), 0.27)
    ts(("Li", 22, 24), ("Li", 10, 12), 4, 1, Op.arith_shift_right, Op.bitwise_and)
    ts(("Li", 21, 22), ("Li", 8, 9), 112, None, Op.bitwise_and)
    ts(("Li", 16, 20), ("Li", 0, 4), 15, None, Op.bitwise_and)
    ts(("Li", 20, 21), ("Li", 4, 5), 112, None, Op.bitwise_and)
    cp(("L", 16 * OC, 16 * OC + 8), ("Li", 16, 24))
    kcol, gcol = col(OC, 0), col(OC, 4)
    ts(col(OC, 8), col(OC, 6), 272.0, col(OC, 5), Op.mult, Op.add)
    cp(("q0", 256, 272), ("w0i", 0, 16))
    ts(("Lu", 0, 16), Lf(J2), col(OC, 8), col(OC, 7), Op.add, Op.add)
    ts(IF, ("J", 0, 128), kcol, gcol, Op.subtract, Op.is_equal)
    ts(("Wb", 0, 128), ("J", 0, 128), gcol, None, Op.is_equal)
    ts(Lf(NUM), ("J", 0, 16), 16.0, kcol, Op.mult, Op.add)
    ts(BD, ("Gm", 0, 128), gcol, None, Op.is_equal)
    ts(Lf(W1), ("w0i", 0, 16), K + 1 - 16 * LOW, None, Op.add)
    ts(("L", 16 * SC, 16 * SC + 4), ("L", 16 * OC, 16 * OC + 4), -BIG, K - BIG, Op.mult, Op.add)
    made = set()

    def rows_col(i, n, val, add, k=None):
        if not n:
            return add
        c = col(i, len([m for m in made if m[0] == i and m < (i, n, val, add)]))
        for m in made:
            if m[:4] == (i, n, val, add):
                return m[4]
        c = col(i, len([m for m in made if m[0] == i]))
        made.add((i, n, val, add, c))
        ts(c, kcol, 4.0 * n, val, Op.is_lt, Op.mult)
        act(c, c, Fn.Identity, add)
        return c

    act(("thf", 0, H), ("J", 0, H), Fn.Exp, 64 * LNB + math.log(2.55), -LNB, 1.3)
    act(IB, IF, Fn.Copy)
    act(("Ib", 128, 256), IF, Fn.Copy)

    def more_constants():
        act(("Wb", 128, 256), ("Wb", 0, 128), Fn.Copy)
        act(("Wb", 256, 320), ("Wb", 0, 64), Fn.Copy)
        act(NIB, IF, Fn.Copy, 0.0, -1.0)
        act(BIB, IF, Fn.Copy, 0.0, BIG)
        act(col(SC, RO), col(SC, RO), Fn.Identity, 1.0)
        act(Lf(WC, 0), Lf(NUM, 0), Fn.Exp, 64 * LNB, -LNB)
        act(("thr", 0, H), ("thf", 0, H), Fn.Copy)
        act(("Wl", 0, 256), ("Wb", 0, 256), Fn.Copy, 0.0, -BIG / 16)
        act(Lf(DUM), Lf(NUM), Fn.Identity, BIG)

    def order_of_rows(t):
        tq = ("Tq", 128 * (t - 1), 128 * t)
        ts(tq, ("Km", 16 - t, 144 - t), col(OC, t), -BIG, Op.is_gt, Op.mult)
        tt(("Tri", 128 * (t - 1), 128 * t), tq, BD, Op.mult)

    def ch(name, h, c, n=1):
        return (name, 2048 * h + 512 * c, 2048 * h + 512 * (c + n))

    def row(name, h, k):
        return (name, 2048 * h + H * k, 2048 * h + H * k + H)

    def hf(name, h, at=0):
        return (name, at + H * h, at + H * h + H)

    def reg(a, n=H):
        return ("P", a, a + n)

    def PB(c, n=1):
        return reg(2048 + 512 * c, 512 * n)

    CN = {F: reg(0), S: reg(1536)}
    ZL = {F: reg(128, 8), S: reg(1664, 8)}
    KR = {F: reg(256), S: reg(1792)}
    CG = {F: reg(512), S: reg(640)}
    CL = {F: reg(896), S: reg(768)}
    VAL = {F: reg(1024), S: reg(0)}
    NR = {F: reg(1152), S: reg(384)}
    WL = reg(512, 16)

    def ship(t):
        send(relay_of(core, T, topo), ("Gh", V * (t - 2), V * (t - 1)), ("Rh", V * (t - 2), V * (t - 1)), "tin%d" % t, "sent",
             2 * TABLE, fold_es, "tb%d" % t)

    def narrowed(t, q):
        for lo, hi in ((0, V // 2), (V // 2, V)):
            copy_on(q, ("Rh", V * (t - 2) + lo, V * (t - 2) + hi), ("R", K + lo, K + hi))

    def widened(t):
        for lo, hi in ((0, V // 2), (V // 2, V)):
            copy_on("g", ("G%d" % t, K + lo, K + hi), ("Gh", V * (t - 2) + lo, V * (t - 2) + hi))

    def step(t):
        s = t - 1
        now[0] = t
        last = t == RO
        q, qn = "q%d" % s, "q%d" % t
        A = "A%d" % (s % 2)
        guest, asker = T.cores[(rank + t) % N], T.cores[(rank - t) % N]
        lq0 = 272 * s
        asked, GW = ("lq", RW) if t == 1 else ("qs", ("G%d" % t, K, K + V))
        new, goal = ("up", lq0, lq0 + K), ("up", lq0 + K, lq0 + 272)

        def spread(e, name, h):
            if h:
                copy_on(e, (name, 640, 768), (name, 512, 640))
                copy_on(e, (name, 768, 1024), (name, 512, 768))
            else:
                copy_on(e, (name, 256, 384), (name, 384, 512))
                copy_on(e, (name, 0, 256), (name, 256, 512))

        def tally(out, d, h, chunks, back, close):
            ks = [k for c in chunks for k in range(4 * c, 4 * c + 4)]
            for i, k in enumerate(ks):
                mm(out, Ek("Wb", k - back), row(d, h, k), i == 0, close and i == 15)

        def likeness(d, h, names, o, wide, narrow, ns, out, back):
            def test(c):
                if c < ns:
                    ts(ch(d, h, c), PB(bank[c]), C4, C4, Op.add, Op.is_equal)
                else:
                    ts(ch(d, h, c), ch(d, h, c), C4, C4, Op.add, Op.is_equal)

            bank, table = {}, GW if d == "dG" else RW
            for c in range(ns):
                bank[c] = turn[0] % 4
                turn[0] += 1
                got = ("gh", 512 * bank[c], 512 * bank[c] + 512)
                pick(got, table, (names, o + 32 * c, o + 32 * c + 32), "a")
                mm(PB(bank[c]), IB, got, True, False)
                for i in range(4):
                    mm(reg(PB(bank[c])[1] + H * i), NIB, hf(wide, h, 384), False, i == 3)
            done = []
            for c in range(ns, 4):
                if c < ns + narrow:
                    for k in range(4 * c, 4 * c + 4):
                        pick_less(row(d, h, k), table, (names, o + 8 * k, o + 8 * k + 8), hf(wide, h, 384))
                else:
                    pick_less(ch(d, h, c), table, (names, o + 32 * c, o + 32 * c + 32), (wide, 512 * h, 512 * h + 512))
                for e in ([c - 1] if c > ns else []) + ([c - ns] if c - ns < ns else []):
                    test(e)
                    done.append(e)
            for c in [c for c in range(4) if c not in done]:
                test(c)
                done.append(c)
            tally(out, d, h, done, back, d == "dG")

        def serve(h):
            ns = OPT["ns_guest"][s][h]
            likeness("dG", h, asked, lq0 + H * h, "G4", OPT["gnarrow"] if h == F or t == 1 else 0, ns, CG[h], 16 * t)
            if t == 1:
                act(hf("an", h), CG[h], Fn.Sign, -11.5)
                send(asker, hf("la", h), hf("an", h), "aa%d" % h)
            else:
                act(hf("la", h, K * s), CG[h], Fn.Sign, -11.5)

        def choose(h):
            ns = 0
            mm(VAL[h], IB, hf("R4", h, 384) if last else hf("nn", h), True, False)
            mm(CN[h], BIB, hf("la", h, K * s), False, True)
            if OPT["twin"][h] == "a":
                act(hf("twin", h), CN[h], Fn.Sign, rows_col(CO, ns, 4.0, -BIG - 11.5))
                shift = col(SC, t)
            else:
                ts(hf("twin", h), CN[h], rows_col(CO, ns, -4.0, BIG + 11.5), 2.0, Op.is_ge, Op.mult)
                shift = K + last - 2 * BIG
            mm(VAL[h], BIB, hf("twin", h), False, False)
            mm(VAL[h], ("Tri", 128 * s, 128 * s + 128), hf("twin", h), False, True)
            ts(hf("sel", h), VAL[h], shift, -LOW, Op.add, Op.max)
            for r in range(16):
                mm(ZL[h], Ek("Wb", r), ("sel", H * h + r, H * h + H), r == 0, r == 15, 16)
            if not last:
                mm(KR[h], BD, hf("sel", h), True, True)
            j, jm, z = ("Li", 32 + 8 * h, 40 + 8 * h), ("Li", 48 + 8 * h, 56 + 8 * h), (qn, 256 + 8 * h, 264 + 8 * h)
            tt(j, ZL[h], Lf(W1, h), Op.max)
            ts(jm, j, 2047, None, Op.bitwise_and)
            ts(z, jm, float(K), float(K), Op.max, Op.subtract)
            pick(hf("xz", h), XZ, z, OPT["xz"][h])
            if not last:
                ts(Lf(KEY, h), ZL[h], 15 * LOW, None, Op.add)
                ts(hf("key", h), KR[h], 15 * LOW, None, Op.add)

        def differ(h, c):
            mm(PB(c), IB, ch("XC", h, c), True, False)
            for i in range(4):
                mm(reg(PB(c)[1] + H * i), NIB, hf("xz", h), False, i == 3)

        def differs(h):
            n = OPT["near"][h]
            if h == F:
                for c in (0, 2):
                    differ(F, c)
                    differ(F, c + 1)
                    act(ch(A, F, c, 2), PB(c, 2), Fn.Abs)
                return
            for c in list(range(n)) + list(range(n, 4)):
                differ(S, c)
                if c >= n:
                    ts(ch("nr", S, c), PB(c), C1, C1, Op.add, Op.is_equal)
                if c == n - 1:
                    act(ch(A, S, 0, n), PB(0, n), Fn.Abs)

        def near(h):
            n = OPT["near"][h]
            if n:
                act(ch("nr", h, 0, n), ch(A, h, 0, n), Fn.Sign, 0.5 + 2.0 ** -20, -1.0)

        def near_first():
            n = OPT["near"][F]
            for c in range(4 - n):
                ts(ch("nr", F, c), ch(A, F, c), 0.5, None, Op.is_le)
            for c, m in {0: [], 1: [(3, 1)], 2: [(2, 2)], 3: [(1, 1), (2, 2)], 4: [(0, 2), (2, 2)]}[n]:
                act(ch("nr", F, c, m), ch(A, F, c, m), Fn.Sign, 0.5 + 2.0 ** -20, -1.0)

        def near_count(h):
            n = OPT["near"][h]
            if h == F:
                return tally(NR[h], "nr", h, range(4), 0, True)
            tally(NR[h], "nr", h, [n] + list(range(n)) + list(range(n + 1, 4)) if n < 4 and h == S else
                  list(range(n, 4)) + list(range(n)), 0, True)

        def claims(h):
            mm(CL[h], NIB, ("thr", 0, H), True, False)
            for b in range(8):
                n = H - 16 * b
                at = 576 * h + sum(H - 16 * i for i in range(b))
                e = ("eq", at, at + n)
                ts(e, ("key", H * h + 16 * b, H * h + H), col(KEY, 8 * h + b), col(WC, b), Op.is_equal, Op.mult)
                mm(("P", CL[h][2] - n, CL[h][2]), BD, e, False, b == 7)

        def put(h):
            pick_less(hf("dl", h), RW, (qn, 256 + 8 * h, 264 + 8 * h), hf("nn", h))
            n = OPT["near"][h]
            bound = rows_col(CB, n, -6.0, 9.5) if h == S else rows_col(CB, 4 - n, 6.0, 3.5)
            ts(NR[h], NR[h], bound, None, Op.is_lt)
            tt(NR[h], NR[h], hf("dl", h), Op.mult)
            tt(hf("up", h, lq0), NR[h], hf("nn", h), Op.add)

        def write(table, name, at, to):
            ts(("Lu", to, to + 16), (name, at + K, at + 272), -BIG, None, Op.add)
            for h in (F, S):
                off, src = ("Lu", to + 8 * h, to + 8 + 8 * h), hf(name, h, at)
                op("v", [src, off], [(table, 0, 2048)],
                   lambda e, off=off, src=src: e.tensor_copy(T[table][:, :].indirect(ap(off)), ap(src)),
                   0.05 + SCATTER * H * CYCLE)

        def expo(h, c, n=1):
            act(ch(A, h, c, n), ch(A, h, c, n), Fn.Exp, 0.0, -1.0)

        def fold(h):
            rid, pid = topo.addr(helper, core)
            es = fold_es if h == F else [e for e in topo.engines(core, helper) if e not in fold_es]
            trs = [RemoteDMATransfer(dst_ids=[DstId(rid=rid, pnc=pid)], dma_engine_mask=bits(es),
                                     remote_sem=T.sem["hin%d" % (2 * s + h)], srcs=[ap(row(A, h, k)) for k in range(16)],
                                     dsts=[ap(hf("ss", h, K * s))], alu_op=1)]
            job("g", [ch(A, h, 0, 4)], [("far", len(far), len(far) + 1)],
                lambda e: e.remote_dma_fused(trs, local_sem=T.sem["fold%d" % (2 * s + h)]), ISSUE, "fold%d" % (2 * s + h),
                len(es), FOLD + FAR, True)
            lands("back%d" % (2 * s + h), len(topo.engines(helper, core)), [hf("ss", h, K * s)])
            if h == S:
                ss = ("ss", K * s, K * s + K)
                dma([ss], [], T.y[:, K * s:K * s + K], ap(ss), 0.3)

        pick(("Rw", 16, 272), RW, (q, 256, 272))
        flip(("Tr", 256, 544), ("Rw", 0, 288))
        flip(("Tr", 0, 256), ("Rw", 16, 272))
        pick(("qh", 0, 256), ("Tr", 0, 544), ("Lu", 0, 16))
        mm(reg(1536, K), ("Ib", 128 - 16 * t, 256 - 16 * t), ("qh", 0, K), True, True)
        cp(("qs", lq0, lq0 + K), reg(1536, K))
        cp((q, 0, 256), ("qh", 0, 256))
        copy_on(OPT["spread"][4], ("R4", 384, 640), ("Rw", 16, 272))
        if OPT["ns_own"][s][F] + OPT["narrow"] < 4:
            spread(OPT["spread"][0], "R4", F)
        if t == 1:
            send(guest, ("lq", 0, K), ("qs", 0, K), "qa0")
            ship(2)
            act(("Xs", 15 + V, 16 + V), ("Xs", 15, 16), Fn.Copy)
            cp(("lq", K, K + 16), ("w0g", 16, 32))
        else:
            write("G%d" % t, "lu", lq0 - 272, 32)
        if t == 2:
            narrowed(3, "g")
            ship(3)
        while early:
            early.pop(0)()
        pick(("G4", 384, 640), GW, (asked, lq0 + 256, lq0 + 272))
        if OPT["ns_guest"][s][F] + OPT["gnarrow"] < 4:
            spread(OPT["spread"][1], "G4", F)
        while late:
            late.pop(0)()
        if t == 1:
            spread(OPT["spread"][2], "R4", S)
        if OPT["ns_guest"][s][S] + (OPT["gnarrow"] if t == 1 else 0) < 4:
            spread(OPT["spread"][3], "G4", S)
        if t > 1:
            spread(OPT["spread"][2], "R4", S)
        if not last:
            iota(("G%d" % (t + 1), 0, K), [[0, K]], 0, 0)
        if not last:
            act(("rr", 0, K), ("Rw", 16, 272), Fn.Relu, -float(V * (V - 2)), float(V))
            mm(reg(512, K), IB, ("R4", 384, 640), True, False)
            mm(reg(512, K), NIB, ("rr", 0, K), False, True)
            act(("nn", 0, K), reg(512, K), Fn.Identity, 1.0)
        def states(h):
            for c in range(4):
                pick(ch("XC", h, c), XW, (q, H * h + 32 * c, H * h + 32 * c + 32), "a")

        if t == 1:
            serve(F)
        likeness("dO", F, q, H * F, "R4", OPT["narrow"], OPT["ns_own"][s][F], CN[F], 0)
        while late:
            late.pop(0)()
        serve(S if t == 1 else F)
        if t == 1:
            order_of_rows(1)
        choose(F)
        states(F)
        if t > 1:
            serve(S)
        states(S)
        likeness("dO", S, q, H * S, "R4", 0, OPT["ns_own"][s][S], CN[S], 0)
        if t == 1:
            for i in range(2, RO + 1):
                order_of_rows(i)
        if not last:
            widened(t + 1)
            differs(F)
            choose(S)
            differs(S)
            near(S)
            claims(F)
            near_first()
            ts(("qh", 256, 272), ("Li", 48, 64), float(K), float(K), Op.max, Op.subtract)
            mm(reg(1920, 16), ("Ib", 112 - 16 * t, 240 - 16 * t), ("qh", 256, 272), True, True)
            cp(("qs", lq0 + 528, lq0 + 544), reg(1920, 16))
            claims(S)
            act(("win", 0, K), reg(768, K), Fn.Sign)
            near_count(F)
            near_count(S)
            mm(WL, IF, Lf(KEY), True, False)
            for r in range(16):
                mm(WL, Ek("Wl", r), ("win", r, K), False, r == 15, 16)
            put(F)
            tt(goal, WL, Lf(DUM), Op.max)
            put(S)
            ts(Lf(W1), ("Li", 48, 64), float(K), 1 - 16 * LOW, Op.max, Op.add)
            send(T.cores[(rank - t - 1) % N], ("lu", lq0, lq0 + 272), ("up", lq0, lq0 + 272), "up%d" % t)
            write("R", "up", lq0, 16)
            n = OPT["near"][S]
            behind("a", lambda: [act(ch(A, S, n, 4 - n), PB(n, 4 - n), Fn.Abs)] + [expo(F, c, 2) for c in (0, 2)])
            early.append(lambda: fold(F))
            late.extend([lambda c=c: expo(S, c, 2) for c in (0, 2)] + [lambda: fold(S)])
        else:
            SUM = NR[F]
            for c in (0, 2):
                differ(F, c)
                differ(F, c + 1)
                act(ch(A, F, c, 2), PB(c, 2), Fn.Abs)
            choose(S)
            expo(F, 0, 2)
            act(PB(2, 2), ch(A, F, 2, 2), Fn.Exp, 0.0, -1.0)
            a, b = ch(A, F, 2)[1], PB(2)[1]
            tt((A, a, a + 512), PB(3), ch(A, F, 1), Op.add)
            tt(PB(2), PB(2), ch(A, F, 0), Op.add)
            tt((A, a + 512, a + 768), reg(b + K, K), (A, a + K, a + 512), Op.add)
            tt(reg(1152, K), reg(b, K), (A, a, a + K), Op.add)
            for c in (0, 1, 3, 2):
                differ(S, c)
            act(ch(A, S, 0, 2), PB(0, 2), Fn.Abs)
            for c in (3, 2):
                ts(("acc", 0, 512), PB(c), -1.0, None, Op.mult)
                tt(ch(A, S, c), PB(c), ("acc", 0, 512), Op.max)
            tt((A, a, a + H), reg(1152), (A, a + 512, a + 640), Op.add)
            tt(reg(1152), reg(1280), (A, a + 640, a + 768), Op.add)
            tt(hf("yo", F), reg(1152), (A, a, a + H), Op.add)
            expo(S, 0, 2)
            for k in range(8):
                mm(NR[S], IF, row(A, S, k), k == 0, k == 7)
            expo(S, 2)
            act(PB(3), ch(A, S, 3), Fn.Exp, 0.0, -1.0)
            a, b = ch(A, S, 2)[1], PB(3)[1]
            tt(("acc", 0, K), reg(b, K), (A, a, a + K), Op.add)
            tt(reg(b + K, K), reg(b + K, K), (A, a + K, a + 2 * K), Op.add)
            tt(("acc", K, K + H), reg(b + K), ("acc", 0, H), Op.add)
            tt(reg(b), reg(b + K + H), ("acc", H, K), Op.add)
            tt(("acc", K, K + H), reg(b), ("acc", K, K + H), Op.add)
            tt(hf("yo", S), NR[S], ("acc", K, K + H), Op.add)
            dma([("yo", 0, K)], [], T.y[:, K * s:K * s + K], T.yo[:, :], 0.3)

    narrowed(2, "a")
    more_constants()
    for t in range(1, RO + 1):
        step(t)
    return jobs
